import numpy as np
import ml_dtypes


def mxq(x, axis, fmt="e4m3"):
    dtype, down = {"e4m3": (ml_dtypes.float8_e4m3fn, 7), "e5m2": (ml_dtypes.float8_e5m2, 14)}[fmt]
    v = np.moveaxis(np.asarray(x, np.float32).astype(ml_dtypes.bfloat16).astype(np.float64), axis, -1)
    blocks = v.reshape(v.shape[:-1] + (-1, 32))
    amax = np.abs(blocks).max(-1, keepdims=True)
    byte = np.maximum(np.where(amax > 0, np.frexp(amax)[1] - 1 + 127, 0) - down, 1)
    scale = np.exp2(byte - 127.0)
    codes = (blocks / scale).astype(np.float32).astype(dtype).astype(np.float64)
    return np.moveaxis((codes * scale).reshape(v.shape), -1, axis)


WIDE = False


def mx_kscale(k):
    if not WIDE:
        return np.ones(k)
    levels = np.array([10, -10, 5, -5, 0])
    if k % 512:
        return np.exp2(np.random.permutation(np.resize(levels, k // 32))).repeat(32)
    a = np.empty((k // 512, 16))
    for p in range(k // 512):
        a[p, :8] = np.random.permutation(np.resize(levels, 8))
        for g in range(8):
            far = levels[np.abs(levels - a[p, g]) >= 10]
            a[p, g + 8] = far[np.random.randint(len(far))]
    return np.exp2(a.ravel()).repeat(32)


def f64(x):
    return np.asarray(x).astype(np.float64)


def striped(idx):
    return np.tile(idx.reshape(-1, 16).T, (8, 1)).astype(np.uint16)


def unstriped(offs):
    return offs[:16].T.reshape(-1).astype(np.int64)


def pack_weight(w):
    k, n = w.shape
    w = f64(np.asarray(w, np.float32).astype(ml_dtypes.bfloat16)).reshape(k // 32, 32, n)
    amax = np.abs(w).max(1)
    byte = np.clip(np.where(amax > 0, np.frexp(amax)[1] - 1 + 127 - 7, 1), 1, 254)
    scaled = (w * np.exp2(127.0 - byte)[:, None, :]).reshape(k, n).astype(np.float32)
    words = np.ascontiguousarray(scaled.reshape(k // 512, 128, 4, n).transpose(0, 1, 3, 2)).astype(ml_dtypes.float8_e4m3fn).view(np.uint8)
    return words, np.ascontiguousarray(byte.astype(np.uint8).reshape(k // 512, 16, n))


def unpack_weight(words, scales):
    g, p, n, _ = words.shape
    vals = np.ascontiguousarray(words).view(ml_dtypes.float8_e4m3fn).astype(np.float64) * np.repeat(np.exp2(scales.astype(np.float64) - 127.0), 8, axis=1)[..., None]
    return vals.transpose(0, 1, 3, 2).reshape(g * 512, n)


def relu2(v):
    return np.maximum(v, 0.0) ** 2


K, T, S, H, N = 1536, 1024, 512, 512, 128


def setup_inputs():
    n = np.random.standard_normal
    s = mx_kscale(K)[:, None]
    u = mx_kscale(H)
    packed = pack_weight(n((K, T)) * s)
    return {
        "x_words": packed[0],
        "x_scales": packed[1],
        "w1": (n((K, H)) / np.sqrt(K) / s * u).astype(np.float32),
        "w2": (n((H, N)) / np.sqrt(H) / u[:, None] ** 2).astype(np.float32),
        "offs": striped(np.random.permutation(T)[:S]),
    }


def reference(x_words, x_scales, w1, w2, offs):
    idx = unstriped(offs)
    xq = unpack_weight(x_words, x_scales)[:, idx]
    h = relu2(mxq(f64(w1), 0, "e4m3").T @ xq)
    y = mxq(f64(w2), 0, "e4m3").T @ mxq(h, 0, "e4m3")
    return y

@@ -1,0 +1,183 @@
+from contextlib import ExitStack
+
+import concourse.mybir as mybir
+
+K, T, S, H, N = 1536, 1024, 512, 512, 128
+FLOPS = 2 * K * H * S + 2 * H * N * S
+
+F32 = mybir.dt.float32
+BF16 = mybir.dt.bfloat16
+I32 = mybir.dt.int32
+U32 = mybir.dt.uint32
+U16 = mybir.dt.uint16
+U8 = mybir.dt.uint8
+FP8X4 = mybir.dt.float8_e4m3fn_x4
+ACT = mybir.ActivationFunctionType
+ALU = mybir.AluOpType
+
+P = 128
+PACK = 4
+PASSES = K // (P * PACK)
+HALF = S // 2
+CHUNK = 128
+
+
+def tile_picked_pick_mlp_relu2_sub_p_kernel(tc, x_words, x_scales, w1, w2, offs, out):
+    nc = tc.nc
+    with ExitStack() as ctx:
+        keep = ctx.enter_context(tc.tile_pool(name="keep", bufs=1))
+        psum = ctx.enter_context(tc.psum_pool(name="psum", bufs=1))
+
+        offsets = keep.tile([P, S // 16], U16, name="offsets")
+        xs_all = keep.tile([P, T // 4], I32, name="xs_all", tag="xs_all", align_bytes=64)
+        xw_all = [keep.tile([P, T], I32, name=f"xw_all{g}", tag=f"xw_all{g}", align_bytes=64) for g in range(PASSES)]
+        w1_raw = [keep.tile([P, PACK, H], F32, name=f"w1_raw{g}", tag=f"w1_raw{g}", align_bytes=64) for g in range(2)]
+        w1_last = [keep.tile([P, 2, H], F32, name=f"w1_last{u}", tag=f"w1_last{u}", align_bytes=64) for u in range(2)]
+        w1_bf = [keep.tile([P, PACK * H], BF16, name=f"w1_bf{g}", tag=f"w1_bf{g}", align_bytes=64) for g in range(2)]
+        xw = []
+        w1_codes = [keep.tile([P, H], U32, name=f"w1_codes{g}", align_bytes=64) for g in range(PASSES)]
+        w1_scales = [keep.tile([P, H], U8, name=f"w1_scales{g}", align_bytes=64) for g in range(PASSES)]
+        w2_raw = keep.tile([P, PACK, N], F32, name="w2_raw")
+        w2_codes = keep.tile([P, N], U32, name="w2_codes", align_bytes=64)
+        w2_scales = keep.tile([P, N], U8, name="w2_scales", align_bytes=64)
+
+        def w1_rows(g):
+            return w1[g * 512 : (g + 1) * 512, :].rearrange("(p j) c -> p j c", j=PACK)
+
+        def load_x(g):
+            nc.sync.dma_start(out=xw_all[g][:], in_=x_words[g].rearrange("p c r -> p (c r)").bitcast(I32))
+
+        nc.gpsimd.memset(xs_all[:], 0)
+        nc.sync.dma_start(out=w1_raw[0][:], in_=w1_rows(0))
+        nc.sync.dma_start(offsets[:], offs)
+        for q in range(4):
+            nc.gpsimd.dma_start(out=xs_all[32 * q : 32 * q + 4 * PASSES, :], in_=x_scales[:, 4 * q : 4 * q + 4, :].bitcast(I32))
+        load_x(0)
+        nc.sync.dma_start(out=w1_raw[1][:], in_=w1_rows(1))
+        load_x(1)
+        for u in range(2):
+            nc.sync.dma_start(out=w1_last[u][:], in_=w1_rows(2)[:, 2 * u : 2 * u + 2, :])
+        load_x(2)
+        nc.sync.dma_start(out=w2_raw[:], in_=w2.rearrange("(p j) m -> p j m", j=PACK))
+
+        def cast_w1(g, raw, j0, split):
+            jn = raw.shape[1]
+            dst = w1_bf[g][:].rearrange("p (t m j) -> p m j t", t=PACK, j=PACK)[:, :, j0 : j0 + jn, :]
+            src = raw[:].rearrange("p j (m t) -> p m j t", t=PACK)
+            if split > 0:
+                nc.scalar.activation(out=dst[:, :split], in_=src[:, :split], func=ACT.Copy)
+            if split < P:
+                nc.vector.tensor_copy(out=dst[:, split:], in_=src[:, split:])
+
+        def quant_w1(g):
+            nc.vector.quantize_mx(out=w1_codes[g][:].bitcast(FP8X4), scales=w1_scales[g][:], in_=w1_bf[g][:])
+
+        def gather_words(g, a, b):
+            nc.vector.tensor_copy(xw[g][:, a:b], xw_all[g][:].bitcast(U32).indirect(offsets[:, a // 16 : b // 16]))
+
+        acc = [[psum.tile([P, HALF], F32, name=f"acc{h}{t}", tag=f"bank{4 * h + t}") for t in range(PACK)] for h in range(2)]
+
+        def layer1(g, h):
+            cols = slice(h * HALF, (h + 1) * HALF)
+            for t in range(PACK):
+                ch = slice(t * P, (t + 1) * P)
+                nc.tensor.matmul_mx(
+                    out=acc[h][t][:],
+                    lhsT=w1_codes[g][:, ch].bitcast(FP8X4),
+                    lhsT_scale=w1_scales[g][:, ch],
+                    rhs=xw[g][:, cols].bitcast(FP8X4),
+                    rhs_scale=xs[4 * g : P, cols],
+                    start=(g == 0),
+                    stop=(g == PASSES - 1),
+                )
+
+        cast_w1(0, w1_raw[0], 0, 48)
+        xw.append(keep.tile([P, S], U32, name="xw0", tag="w1_raw0", align_bytes=64))
+        gather_words(0, 0, S)
+        quant_w1(0)
+        xs = keep.tile([P, S], U8, name="xs", tag="w1_bf0", align_bytes=64)
+        nc.vector.tensor_copy(xs[:], xs_all[:].bitcast(U8).indirect(offsets[:]))
+        layer1(0, 0)
+        layer1(0, 1)
+        cast_w1(1, w1_raw[1], 0, 96)
+        xw.append(keep.tile([P, S], U32, name="xw1", tag="xs_all", align_bytes=64))
+        gather_words(1, 0, S)
+        quant_w1(1)
+        layer1(1, 0)
+        layer1(1, 1)
+        w1_bf.append(keep.tile([P, PACK * H], BF16, name="w1_bf2", tag="xw_all1", align_bytes=64))
+        cast_w1(2, w1_last[0], 0, 80)
+        cast_w1(2, w1_last[1], 2, 48)
+        quant_w1(2)
+        xw.append(keep.tile([P, S], U32, name="xw2", tag="w1_last1", align_bytes=64))
+        gather_words(2, 0, HALF)
+        gather_words(2, HALF, S)
+        layer1(2, 0)
+        layer1(2, 1)
+
+        w2_bf = keep.tile([P, PACK * N], BF16, name="w2_bf", tag="xw_all1", align_bytes=64)
+        nc.scalar.activation(
+            out=w2_bf[:].rearrange("p (c i j) -> p c j i", i=4, j=PACK),
+            in_=w2_raw[:].rearrange("p j (c i) -> p c j i", i=4),
+            func=ACT.Copy,
+        )
+
+        pos = [keep.tile([P, PACK, HALF], F32, name=f"pos{h}") for h in range(2)]
+        h_bf = [keep.tile([P, PACK * CHUNK], BF16, name=f"h_bf{q}", align_bytes=64) for q in range(4)]
+        h_codes = [keep.tile([P, CHUNK], U32, name=f"h_codes{q}", align_bytes=64) for q in range(4)]
+        h_scales = [keep.tile([P, CHUNK], U8, name=f"h_scales{q}", align_bytes=64) for q in range(4)]
+        y_sb = [keep.tile([P, CHUNK], F32, name=f"y_sb{q}") for q in range(4)]
+
+        def relu(h, t, on_scalar):
+            if on_scalar:
+                nc.scalar.activation(out=pos[h][:, t, :], in_=acc[h][t][:], func=ACT.Relu)
+            else:
+                nc.vector.tensor_scalar_max(pos[h][:, t, :], acc[h][t][:], 0.0)
+
+        def square(q, on_scalar):
+            n0 = (q % 2) * CHUNK
+            src = pos[q // 2][:, :, n0 : n0 + CHUNK].rearrange("p t (c i) -> p c t i", i=4)
+            dst = h_bf[q][:].rearrange("p (c i t) -> p c t i", i=4, t=PACK)
+            if on_scalar:
+                nc.scalar.activation(out=dst, in_=src, func=ACT.Square)
+            else:
+                nc.vector.tensor_tensor(dst, src, src, ALU.mult)
+
+        def quant_h(q):
+            nc.vector.quantize_mx(out=h_codes[q][:].bitcast(FP8X4), scales=h_scales[q][:], in_=h_bf[q][:])
+
+        def layer2(q):
+            y = psum.tile([P, CHUNK], F32, name=f"y{q}", tag=f"bank{q}")
+            nc.tensor.matmul_mx(
+                out=y[:],
+                lhsT=w2_codes[:].bitcast(FP8X4),
+                lhsT_scale=w2_scales[:],
+                rhs=h_codes[q][:].bitcast(FP8X4),
+                rhs_scale=h_scales[q][:],
+                start=True,
+                stop=True,
+            )
+            nc.scalar.activation(out=y_sb[q][:], in_=y[:], func=ACT.Copy)
+            nc.sync.dma_start(out=out[:, q * CHUNK : (q + 1) * CHUNK], in_=y_sb[q][:])
+
+        relu(0, 0, True)
+        relu(0, 1, True)
+        relu(0, 2, False)
+        relu(0, 3, False)
+        nc.vector.quantize_mx(out=w2_codes[:].bitcast(FP8X4), scales=w2_scales[:], in_=w2_bf[:])
+        square(0, True)
+        relu(1, 0, False)
+        relu(1, 1, False)
+        square(1, True)
+        quant_h(0)
+        relu(1, 2, False)
+        relu(1, 3, False)
+        layer2(0)
+        quant_h(1)
+        square(2, True)
+        square(3, False)
+        layer2(1)
+        quant_h(2)
+        quant_h(3)
+        layer2(2)
+        layer2(3)

@@ -28,18 +28,26 @@ def tile_picked_pick_mlp_relu2_sub_p_kernel(tc, x_words, x_scales, w1, w2, offs,
         keep = ctx.enter_context(tc.tile_pool(name="keep", bufs=1))
         psum = ctx.enter_context(tc.psum_pool(name="psum", bufs=1))
 
+        reuse = ctx.enter_context(tc.tile_pool(name="reuse", bufs=1))
+
+        def placed(name, shape, dtype, kib):
+            return reuse.tile(shape, dtype, name=name, tag=name, align_bytes=64, offset=int(1024 * kib))
+
         offsets = keep.tile([P, S // 16], U16, name="offsets")
-        xs_all = keep.tile([P, T // 4], I32, name="xs_all", tag="xs_all", align_bytes=64)
-        xw_all = [keep.tile([P, T], I32, name=f"xw_all{g}", tag=f"xw_all{g}", align_bytes=64) for g in range(PASSES)]
-        w1_raw = [keep.tile([P, PACK, H], F32, name=f"w1_raw{g}", tag=f"w1_raw{g}", align_bytes=64) for g in range(2)]
-        w1_last = [keep.tile([P, 2, H], F32, name=f"w1_last{u}", tag=f"w1_last{u}", align_bytes=64) for u in range(2)]
-        w1_bf = [keep.tile([P, PACK * H], BF16, name=f"w1_bf{g}", tag=f"w1_bf{g}", align_bytes=64) for g in range(2)]
-        xw = []
         w1_codes = [keep.tile([P, H], U32, name=f"w1_codes{g}", align_bytes=64) for g in range(PASSES)]
         w1_scales = [keep.tile([P, H], U8, name=f"w1_scales{g}", align_bytes=64) for g in range(PASSES)]
-        w2_raw = keep.tile([P, PACK, N], F32, name="w2_raw")
         w2_codes = keep.tile([P, N], U32, name="w2_codes", align_bytes=64)
         w2_scales = keep.tile([P, N], U8, name="w2_scales", align_bytes=64)
+
+        xs_all = keep.tile([P, T // 4], I32, name="xs_all", align_bytes=64)
+        w1_raw = [placed("w1_raw0", [P, PACK, H], F32, 16), placed("w1_raw1", [P, PACK, H], F32, 0)]
+        w1_last = [placed("w1_last0", [P, 2, H], F32, 10), placed("w1_last1", [P, 2, H], F32, 16)]
+        xw_all = [placed("xw_all0", [P, T], I32, 7), placed("xw_all1", [P, T], I32, 27), placed("xw_all2", [P, T], I32, 24)]
+        w1_bf = [placed("w1_bf0", [P, PACK * H], BF16, 32), placed("w1_bf1", [P, PACK * H], BF16, 36), placed("w1_bf2", [P, PACK * H], BF16, 0)]
+        xw = [placed("xw0", [P, S], U32, 40), placed("xw1", [P, S], U32, 20), placed("xw2", [P, S], U32, 16)]
+        xs = placed("xs", [P, S], U8, 22)
+        w2_raw = placed("w2_raw", [P, PACK, N], F32, 30)
+        w2_bf = placed("w2_bf", [P, PACK * N], BF16, 0)
 
         def w1_rows(g):
             return w1[g * 512 : (g + 1) * 512, :].rearrange("(p j) c -> p j c", j=PACK)
@@ -47,18 +55,16 @@ def tile_picked_pick_mlp_relu2_sub_p_kernel(tc, x_words, x_scales, w1, w2, offs,
         def load_x(g):
             nc.sync.dma_start(out=xw_all[g][:], in_=x_words[g].rearrange("p c r -> p (c r)").bitcast(I32))
 
-        nc.gpsimd.memset(xs_all[:], 0)
-        nc.sync.dma_start(out=w1_raw[0][:], in_=w1_rows(0))
-        nc.sync.dma_start(offsets[:], offs)
-        for q in range(4):
-            nc.gpsimd.dma_start(out=xs_all[32 * q : 32 * q + 4 * PASSES, :], in_=x_scales[:, 4 * q : 4 * q + 4, :].bitcast(I32))
-        load_x(0)
-        nc.sync.dma_start(out=w1_raw[1][:], in_=w1_rows(1))
-        load_x(1)
-        for u in range(2):
+        def load_last(u):
             nc.sync.dma_start(out=w1_last[u][:], in_=w1_rows(2)[:, 2 * u : 2 * u + 2, :])
-        load_x(2)
-        nc.sync.dma_start(out=w2_raw[:], in_=w2.rearrange("(p j) m -> p j m", j=PACK))
+
+        nc.vector.memset(xs_all[:], 0)
+        nc.sync.dma_start(offsets[:], offs)
+        load_x(0)
+        nc.sync.dma_start(out=w1_raw[0][:], in_=w1_rows(0))
+        load_x(1)
+        for q in range(4):
+            nc.sync.dma_start(out=xs_all[32 * q : 32 * q + 4 * PASSES, :], in_=x_scales[:, 4 * q : 4 * q + 4, :].bitcast(I32))
 
         def cast_w1(g, raw, j0, split):
             jn = raw.shape[1]
@@ -91,31 +97,30 @@ def tile_picked_pick_mlp_relu2_sub_p_kernel(tc, x_words, x_scales, w1, w2, offs,
                     stop=(g == PASSES - 1),
                 )
 
-        cast_w1(0, w1_raw[0], 0, 48)
-        xw.append(keep.tile([P, S], U32, name="xw0", tag="w1_raw0", align_bytes=64))
         gather_words(0, 0, S)
+        nc.sync.dma_start(out=w1_raw[1][:], in_=w1_rows(1))
+        load_last(0)
+        cast_w1(0, w1_raw[0], 0, 56)
+        load_last(1)
+        gather_words(1, 0, S)
+        load_x(2)
+        nc.sync.dma_start(out=w2_raw[:], in_=w2.rearrange("(p j) m -> p j m", j=PACK))
         quant_w1(0)
-        xs = keep.tile([P, S], U8, name="xs", tag="w1_bf0", align_bytes=64)
         nc.vector.tensor_copy(xs[:], xs_all[:].bitcast(U8).indirect(offsets[:]))
         layer1(0, 0)
         layer1(0, 1)
-        cast_w1(1, w1_raw[1], 0, 96)
-        xw.append(keep.tile([P, S], U32, name="xw1", tag="xs_all", align_bytes=64))
-        gather_words(1, 0, S)
+        cast_w1(1, w1_raw[1], 0, 64)
+        cast_w1(2, w1_last[0], 0, 96)
         quant_w1(1)
         layer1(1, 0)
         layer1(1, 1)
-        w1_bf.append(keep.tile([P, PACK * H], BF16, name="w1_bf2", tag="xw_all1", align_bytes=64))
-        cast_w1(2, w1_last[0], 0, 80)
         cast_w1(2, w1_last[1], 2, 48)
         quant_w1(2)
-        xw.append(keep.tile([P, S], U32, name="xw2", tag="w1_last1", align_bytes=64))
         gather_words(2, 0, HALF)
         gather_words(2, HALF, S)
         layer1(2, 0)
         layer1(2, 1)
 
-        w2_bf = keep.tile([P, PACK * N], BF16, name="w2_bf", tag="xw_all1", align_bytes=64)
         nc.scalar.activation(
             out=w2_bf[:].rearrange("p (c i j) -> p c j i", i=4, j=PACK),
             in_=w2_raw[:].rearrange("p j (c i) -> p c j i", i=4),
@@ -161,23 +166,19 @@ def tile_picked_pick_mlp_relu2_sub_p_kernel(tc, x_words, x_scales, w1, w2, offs,
             nc.sync.dma_start(out=out[:, q * CHUNK : (q + 1) * CHUNK], in_=y_sb[q][:])
 
         relu(0, 0, True)
-        relu(0, 1, True)
-        relu(0, 2, False)
+        relu(0, 1, False)
+        relu(0, 2, True)
         relu(0, 3, False)
-        nc.vector.quantize_mx(out=w2_codes[:].bitcast(FP8X4), scales=w2_scales[:], in_=w2_bf[:])
-        square(0, True)
         relu(1, 0, False)
+        relu(1, 2, True)
         relu(1, 1, False)
-        square(1, True)
-        quant_h(0)
-        relu(1, 2, False)
+        square(0, True)
         relu(1, 3, False)
-        layer2(0)
-        quant_h(1)
-        square(2, True)
-        square(3, False)
-        layer2(1)
-        quant_h(2)
-        quant_h(3)
-        layer2(2)
-        layer2(3)
+        nc.vector.quantize_mx(out=w2_codes[:].bitcast(FP8X4), scales=w2_scales[:], in_=w2_bf[:])
+        square(1, True)
+        square(2, False)
+        square(3, True)
+        for q in range(4):
+            quant_h(q)
+        for q in range(4):
+            layer2(q)

@@ -17,9 +17,30 @@ ALU = mybir.AluOpType
 
 P = 128
 PACK = 4
-PASSES = K // (P * PACK)
+K_PASS = P * PACK
+PASSES = K // K_PASS
+LAST = PASSES - 1
+QUADRANT = 32
+SCALE_ROWS = 4
+LIST_ROWS = 16
+LINE = 4
+
 HALF = S // 2
 CHUNK = 128
+CHUNKS = S // CHUNK
+
+LOWER = PACK // 2
+TILE_ORDER = (2, 3, 0, 1)
+SCALAR_CAST_COLUMNS = (112, 112, 96)
+SCALAR_LAST_TOKENS = 40
+
+W1_RAW_KIB = (26, 0, 10)
+WORDS_ALL_KIB = (7, 19, 22)
+W1_BF_KIB = (34, 38, 38)
+WORDS_KIB = (42, 44, 10)
+SCALES_KIB = (46, 34)
+W2_RAW_KIB = 18
+W2_BF_KIB = 12
 
 
 def tile_picked_pick_mlp_relu2_sub_p_kernel(tc, x_words, x_scales, w1, w2, offs, out):
@@ -27,131 +48,163 @@ def tile_picked_pick_mlp_relu2_sub_p_kernel(tc, x_words, x_scales, w1, w2, offs,
     with ExitStack() as ctx:
         keep = ctx.enter_context(tc.tile_pool(name="keep", bufs=1))
         psum = ctx.enter_context(tc.psum_pool(name="psum", bufs=1))
+        placed = ctx.enter_context(tc.tile_pool(name="placed", bufs=1))
 
-        reuse = ctx.enter_context(tc.tile_pool(name="reuse", bufs=1))
+        def kept(name, shape, dtype):
+            return keep.tile(shape, dtype, name=name, align_bytes=64)
 
-        def placed(name, shape, dtype, kib):
-            return reuse.tile(shape, dtype, name=name, tag=name, align_bytes=64, offset=int(1024 * kib))
+        def placed_at(kib, name, shape, dtype):
+            return placed.tile(shape, dtype, name=name, tag=name, align_bytes=64, offset=1024 * kib)
 
-        offsets = keep.tile([P, S // 16], U16, name="offsets")
-        w1_codes = [keep.tile([P, H], U32, name=f"w1_codes{g}", align_bytes=64) for g in range(PASSES)]
-        w1_scales = [keep.tile([P, H], U8, name=f"w1_scales{g}", align_bytes=64) for g in range(PASSES)]
-        w2_codes = keep.tile([P, N], U32, name="w2_codes", align_bytes=64)
-        w2_scales = keep.tile([P, N], U8, name="w2_scales", align_bytes=64)
+        offsets = keep.tile([P, S // LIST_ROWS], U16, name="offsets")
+        w1_codes = [kept(f"w1_codes{g}", [P, H], U32) for g in range(PASSES)]
+        w1_scales = [kept(f"w1_scales{g}", [P, H], U8) for g in range(PASSES)]
+        w2_codes = kept("w2_codes", [P, N], U32)
+        w2_scales = kept("w2_scales", [P, N], U8)
+        scales_all = kept("scales_all", [P, T // 4], I32)
 
-        xs_all = keep.tile([P, T // 4], I32, name="xs_all", align_bytes=64)
-        w1_raw = [placed("w1_raw0", [P, PACK, H], F32, 16), placed("w1_raw1", [P, PACK, H], F32, 0)]
-        w1_last = [placed("w1_last0", [P, 2, H], F32, 10), placed("w1_last1", [P, 2, H], F32, 16)]
-        xw_all = [placed("xw_all0", [P, T], I32, 7), placed("xw_all1", [P, T], I32, 27), placed("xw_all2", [P, T], I32, 24)]
-        w1_bf = [placed("w1_bf0", [P, PACK * H], BF16, 32), placed("w1_bf1", [P, PACK * H], BF16, 36), placed("w1_bf2", [P, PACK * H], BF16, 0)]
-        xw = [placed("xw0", [P, S], U32, 40), placed("xw1", [P, S], U32, 20), placed("xw2", [P, S], U32, 16)]
-        xs = placed("xs", [P, S], U8, 22)
-        w2_raw = placed("w2_raw", [P, PACK, N], F32, 30)
-        w2_bf = placed("w2_bf", [P, PACK * N], BF16, 0)
+        w1_raw = [placed_at(kib, f"w1_raw{g}", [P, PACK, H], F32) for g, kib in enumerate(W1_RAW_KIB)]
+        words_all = [placed_at(kib, f"words_all{g}", [P, T], I32) for g, kib in enumerate(WORDS_ALL_KIB)]
+        w1_bf = [placed_at(kib, f"w1_bf{g}", [P, PACK * H], BF16) for g, kib in enumerate(W1_BF_KIB)]
+        words = [placed_at(kib, f"words{g}", [P, S], U32) for g, kib in enumerate(WORDS_KIB)]
+        scales = [placed_at(kib, f"scales{h}", [P, HALF], U8) for h, kib in enumerate(SCALES_KIB)]
+        w2_raw = placed_at(W2_RAW_KIB, "w2_raw", [P, PACK, N], F32)
+        w2_bf = placed_at(W2_BF_KIB, "w2_bf", [P, PACK * N], BF16)
 
-        def w1_rows(g):
-            return w1[g * 512 : (g + 1) * 512, :].rearrange("(p j) c -> p j c", j=PACK)
+        acc = [
+            [psum.tile([P, HALF], F32, name=f"acc{h}{t}", tag=f"bank{PACK * h + t}") for t in range(PACK)]
+            for h in range(2)
+        ]
 
-        def load_x(g):
-            nc.sync.dma_start(out=xw_all[g][:], in_=x_words[g].rearrange("p c r -> p (c r)").bitcast(I32))
+        def load_words(g):
+            nc.sync.dma_start(out=words_all[g][:], in_=x_words[g].rearrange("p c r -> p (c r)").bitcast(I32))
 
-        def load_last(u):
-            nc.sync.dma_start(out=w1_last[u][:], in_=w1_rows(2)[:, 2 * u : 2 * u + 2, :])
+        def load_w1(g):
+            rows = w1[g * K_PASS : (g + 1) * K_PASS, :]
+            nc.sync.dma_start(out=w1_raw[g][:], in_=rows.rearrange("(p j) c -> p j c", j=PACK))
 
-        nc.vector.memset(xs_all[:], 0)
+        def list_slice(lo, hi):
+            return offsets[:, lo // LIST_ROWS : hi // LIST_ROWS]
+
+        def gather_words(g, lo, hi):
+            nc.vector.tensor_copy(words[g][:, lo:hi], words_all[g][:].bitcast(U32).indirect(list_slice(lo, hi)))
+
+        def gather_scales(h):
+            entries = list_slice(h * HALF, (h + 1) * HALF)
+            nc.vector.tensor_copy(scales[h][:], scales_all[:].bitcast(U8).indirect(entries))
+
+        def cast_w1(g):
+            dst = w1_bf[g][:].rearrange("p (t m j) -> p m j t", t=PACK, j=PACK)
+            src = w1_raw[g][:].rearrange("p j (m t) -> p m j t", t=PACK)
+            split = SCALAR_CAST_COLUMNS[g]
+            nc.scalar.activation(out=dst[:, :split, :, :LOWER], in_=src[:, :split, :, :LOWER], func=ACT.Copy)
+            nc.vector.tensor_copy(out=dst[:, :, :, LOWER:], in_=src[:, :, :, LOWER:])
+            nc.vector.tensor_copy(out=dst[:, split:, :, :LOWER], in_=src[:, split:, :, :LOWER])
+
+        def quantise_w1(g, lo, hi):
+            nc.vector.quantize_mx(
+                out=w1_codes[g][:, lo:hi].bitcast(FP8X4),
+                scales=w1_scales[g][:, lo:hi],
+                in_=w1_bf[g][:, PACK * lo : PACK * hi],
+            )
+
+        def first_product(g):
+            for h in range(2):
+                for t in TILE_ORDER:
+                    channels = slice(t * P, (t + 1) * P)
+                    nc.tensor.matmul_mx(
+                        out=acc[h][t][:],
+                        lhsT=w1_codes[g][:, channels].bitcast(FP8X4),
+                        lhsT_scale=w1_scales[g][:, channels],
+                        rhs=words[g][:, h * HALF : (h + 1) * HALF].bitcast(FP8X4),
+                        rhs_scale=scales[h][SCALE_ROWS * g : P, :],
+                        start=(g == 0),
+                        stop=(g == LAST),
+                    )
+
+        nc.vector.memset(scales_all[:], 0)
+        load_words(0)
         nc.sync.dma_start(offsets[:], offs)
-        load_x(0)
-        nc.sync.dma_start(out=w1_raw[0][:], in_=w1_rows(0))
-        load_x(1)
-        for q in range(4):
-            nc.sync.dma_start(out=xs_all[32 * q : 32 * q + 4 * PASSES, :], in_=x_scales[:, 4 * q : 4 * q + 4, :].bitcast(I32))
-
-        def cast_w1(g, raw, j0, split):
-            jn = raw.shape[1]
-            dst = w1_bf[g][:].rearrange("p (t m j) -> p m j t", t=PACK, j=PACK)[:, :, j0 : j0 + jn, :]
-            src = raw[:].rearrange("p j (m t) -> p m j t", t=PACK)
-            if split > 0:
-                nc.scalar.activation(out=dst[:, :split], in_=src[:, :split], func=ACT.Copy)
-            if split < P:
-                nc.vector.tensor_copy(out=dst[:, split:], in_=src[:, split:])
-
-        def quant_w1(g):
-            nc.vector.quantize_mx(out=w1_codes[g][:].bitcast(FP8X4), scales=w1_scales[g][:], in_=w1_bf[g][:])
-
-        def gather_words(g, a, b):
-            nc.vector.tensor_copy(xw[g][:, a:b], xw_all[g][:].bitcast(U32).indirect(offsets[:, a // 16 : b // 16]))
-
-        acc = [[psum.tile([P, HALF], F32, name=f"acc{h}{t}", tag=f"bank{4 * h + t}") for t in range(PACK)] for h in range(2)]
-
-        def layer1(g, h):
-            cols = slice(h * HALF, (h + 1) * HALF)
-            for t in range(PACK):
-                ch = slice(t * P, (t + 1) * P)
-                nc.tensor.matmul_mx(
-                    out=acc[h][t][:],
-                    lhsT=w1_codes[g][:, ch].bitcast(FP8X4),
-                    lhsT_scale=w1_scales[g][:, ch],
-                    rhs=xw[g][:, cols].bitcast(FP8X4),
-                    rhs_scale=xs[4 * g : P, cols],
-                    start=(g == 0),
-                    stop=(g == PASSES - 1),
-                )
+        load_words(1)
+        load_w1(0)
+        for q in range(P // QUADRANT):
+            nc.sync.dma_start(
+                out=scales_all[QUADRANT * q : QUADRANT * q + SCALE_ROWS * PASSES, :],
+                in_=x_scales[:, SCALE_ROWS * q : SCALE_ROWS * (q + 1), :].bitcast(I32),
+            )
 
         gather_words(0, 0, S)
-        nc.sync.dma_start(out=w1_raw[1][:], in_=w1_rows(1))
-        load_last(0)
-        cast_w1(0, w1_raw[0], 0, 56)
-        load_last(1)
+        load_w1(1)
+        load_w1(2)
         gather_words(1, 0, S)
-        load_x(2)
+        load_words(2)
         nc.sync.dma_start(out=w2_raw[:], in_=w2.rearrange("(p j) m -> p j m", j=PACK))
-        quant_w1(0)
-        nc.vector.tensor_copy(xs[:], xs_all[:].bitcast(U8).indirect(offsets[:]))
-        layer1(0, 0)
-        layer1(0, 1)
-        cast_w1(1, w1_raw[1], 0, 64)
-        cast_w1(2, w1_last[0], 0, 96)
-        quant_w1(1)
-        layer1(1, 0)
-        layer1(1, 1)
-        cast_w1(2, w1_last[1], 2, 48)
-        quant_w1(2)
-        gather_words(2, 0, HALF)
-        gather_words(2, HALF, S)
-        layer1(2, 0)
-        layer1(2, 1)
+
+        cast_w1(0)
+        gather_scales(0)
+        quantise_w1(0, 0, H)
+        gather_scales(1)
+        first_product(0)
+
+        cast_w1(1)
+        quantise_w1(1, 0, H)
+        first_product(1)
+
+        cast_w1(LAST)
+        quantise_w1(LAST, LOWER * P, H)
+        gather_words(LAST, 0, HALF)
+        quantise_w1(LAST, 0, LOWER * P)
+        gather_words(LAST, HALF, S)
+        first_product(LAST)
 
         nc.scalar.activation(
-            out=w2_bf[:].rearrange("p (c i j) -> p c j i", i=4, j=PACK),
-            in_=w2_raw[:].rearrange("p j (c i) -> p c j i", i=4),
+            out=w2_bf[:].rearrange("p (c e j) -> p c j e", e=LINE, j=PACK),
+            in_=w2_raw[:].rearrange("p j (c e) -> p c j e", e=LINE),
             func=ACT.Copy,
         )
 
-        pos = [keep.tile([P, PACK, HALF], F32, name=f"pos{h}") for h in range(2)]
-        h_bf = [keep.tile([P, PACK * CHUNK], BF16, name=f"h_bf{q}", align_bytes=64) for q in range(4)]
-        h_codes = [keep.tile([P, CHUNK], U32, name=f"h_codes{q}", align_bytes=64) for q in range(4)]
-        h_scales = [keep.tile([P, CHUNK], U8, name=f"h_scales{q}", align_bytes=64) for q in range(4)]
-        y_sb = [keep.tile([P, CHUNK], F32, name=f"y_sb{q}") for q in range(4)]
+        positive = [keep.tile([P, PACK, HALF], F32, name=f"positive{h}") for h in range(2)]
+        h_bf = [kept(f"h_bf{q}", [P, PACK * CHUNK], BF16) for q in range(CHUNKS)]
+        h_codes = [kept(f"h_codes{q}", [P, CHUNK], U32) for q in range(CHUNKS)]
+        h_scales = [kept(f"h_scales{q}", [P, CHUNK], U8) for q in range(CHUNKS)]
+        y_sb = [keep.tile([P, CHUNK], F32, name=f"y_sb{q}") for q in range(CHUNKS)]
 
-        def relu(h, t, on_scalar):
-            if on_scalar:
-                nc.scalar.activation(out=pos[h][:, t, :], in_=acc[h][t][:], func=ACT.Relu)
-            else:
-                nc.vector.tensor_scalar_max(pos[h][:, t, :], acc[h][t][:], 0.0)
+        def square_operands(q, lo, hi):
+            h, first = divmod(q * CHUNK, HALF)
+            src = positive[h][:, :, first + lo : first + hi].rearrange("p t (c e) -> p c t e", e=LINE)
+            dst = h_bf[q][:, PACK * lo : PACK * hi].rearrange("p (c e t) -> p c t e", e=LINE, t=PACK)
+            return dst, src
 
-        def square(q, on_scalar):
-            n0 = (q % 2) * CHUNK
-            src = pos[q // 2][:, :, n0 : n0 + CHUNK].rearrange("p t (c i) -> p c t i", i=4)
-            dst = h_bf[q][:].rearrange("p (c i t) -> p c t i", i=4, t=PACK)
-            if on_scalar:
-                nc.scalar.activation(out=dst, in_=src, func=ACT.Square)
-            else:
-                nc.vector.tensor_tensor(dst, src, src, ALU.mult)
+        def square_on_scalar(q, lo, hi):
+            dst, src = square_operands(q, lo, hi)
+            nc.scalar.activation(out=dst, in_=src, func=ACT.Square)
 
-        def quant_h(q):
+        def square_on_vector(q, lo, hi):
+            dst, src = square_operands(q, lo, hi)
+            nc.vector.tensor_tensor(dst, src, src, ALU.mult)
+
+        def quantise_h(q):
             nc.vector.quantize_mx(out=h_codes[q][:].bitcast(FP8X4), scales=h_scales[q][:], in_=h_bf[q][:])
 
-        def layer2(q):
+        for h in range(2):
+            for t in TILE_ORDER:
+                if (h + t) % 2 == 0:
+                    nc.scalar.activation(out=positive[h][:, t, :], in_=acc[h][t][:], func=ACT.Relu)
+                else:
+                    nc.vector.tensor_scalar_max(positive[h][:, t, :], acc[h][t][:], 0.0)
+        nc.vector.quantize_mx(out=w2_codes[:].bitcast(FP8X4), scales=w2_scales[:], in_=w2_bf[:])
+
+        square_on_scalar(0, 0, CHUNK)
+        square_on_vector(1, 0, CHUNK)
+        square_on_scalar(2, 0, CHUNK)
+        square_on_vector(3, SCALAR_LAST_TOKENS, CHUNK)
+        quantise_h(0)
+        quantise_h(1)
+        square_on_scalar(3, 0, SCALAR_LAST_TOKENS)
+        quantise_h(2)
+        quantise_h(3)
+
+        for q in range(CHUNKS):
             y = psum.tile([P, CHUNK], F32, name=f"y{q}", tag=f"bank{q}")
             nc.tensor.matmul_mx(
                 out=y[:],
@@ -162,23 +215,8 @@ def tile_picked_pick_mlp_relu2_sub_p_kernel(tc, x_words, x_scales, w1, w2, offs,
                 start=True,
                 stop=True,
             )
-            nc.scalar.activation(out=y_sb[q][:], in_=y[:], func=ACT.Copy)
+            if q < CHUNKS - 1:
+                nc.scalar.activation(out=y_sb[q][:], in_=y[:], func=ACT.Copy)
+            else:
+                nc.vector.tensor_copy(out=y_sb[q][:], in_=y[:])
             nc.sync.dma_start(out=out[:, q * CHUNK : (q + 1) * CHUNK], in_=y_sb[q][:])
-
-        relu(0, 0, True)
-        relu(0, 1, False)
-        relu(0, 2, True)
-        relu(0, 3, False)
-        relu(1, 0, False)
-        relu(1, 2, True)
-        relu(1, 1, False)
-        square(0, True)
-        relu(1, 3, False)
-        nc.vector.quantize_mx(out=w2_codes[:].bitcast(FP8X4), scales=w2_scales[:], in_=w2_bf[:])
-        square(1, True)
-        square(2, False)
-        square(3, True)
-        for q in range(4):
-            quant_h(q)
-        for q in range(4):
-            layer2(q)

@@ -31,16 +31,21 @@ CHUNKS = S // CHUNK
 
 LOWER = PACK // 2
 TILE_ORDER = (2, 3, 0, 1)
-SCALAR_CAST_COLUMNS = (112, 112, 96)
+SCALAR_UPPER_COLUMNS = (64, 0)
+LAST_SCALAR_COLUMNS = 48
 SCALAR_LAST_TOKENS = 40
 
-W1_RAW_KIB = (26, 0, 10)
-WORDS_ALL_KIB = (7, 19, 22)
-W1_BF_KIB = (34, 38, 38)
-WORDS_KIB = (42, 44, 10)
-SCALES_KIB = (46, 34)
+W1_RAW_KIB = (26, 0)
+LAST_RAW_KIB = (10, 14)
+WORDS_ALL_KIB = (7, 17, 20)
+W1_BF_KIB = ((34, 36), (38, 36))
+W1_CODES_KIB = (52, 54, 56)
+SCALES_ALL_KIB = 53
+LAST_BF_KIB = ((64, 67), (65, 64))
+WORDS_KIB = (42, 44, 16)
+SCALES_KIB = (46, 47)
 W2_RAW_KIB = 18
-W2_BF_KIB = 12
+W2_BF_KIB = 14
 
 
 def tile_picked_pick_mlp_relu2_sub_p_kernel(tc, x_words, x_scales, w1, w2, offs, out):
@@ -54,18 +59,26 @@ def tile_picked_pick_mlp_relu2_sub_p_kernel(tc, x_words, x_scales, w1, w2, offs,
             return keep.tile(shape, dtype, name=name, align_bytes=64)
 
         def placed_at(kib, name, shape, dtype):
-            return placed.tile(shape, dtype, name=name, tag=name, align_bytes=64, offset=1024 * kib)
+            return placed.tile(shape, dtype, name=name, tag=name, align_bytes=64, offset=int(1024 * kib))
 
         offsets = keep.tile([P, S // LIST_ROWS], U16, name="offsets")
-        w1_codes = [kept(f"w1_codes{g}", [P, H], U32) for g in range(PASSES)]
+        w1_codes = [placed_at(kib, f"w1_codes{g}", [P, H], U32) for g, kib in enumerate(W1_CODES_KIB)]
         w1_scales = [kept(f"w1_scales{g}", [P, H], U8) for g in range(PASSES)]
         w2_codes = kept("w2_codes", [P, N], U32)
         w2_scales = kept("w2_scales", [P, N], U8)
-        scales_all = kept("scales_all", [P, T // 4], I32)
 
+        scales_all = placed_at(SCALES_ALL_KIB, "scales_all", [P, T // 4], I32)
         w1_raw = [placed_at(kib, f"w1_raw{g}", [P, PACK, H], F32) for g, kib in enumerate(W1_RAW_KIB)]
+        last_raw = [placed_at(kib, f"last_raw{c}", [P, PACK, H // 2], F32) for c, kib in enumerate(LAST_RAW_KIB)]
+        last_bf = [
+            [placed_at(kib, f"last_bf{c}{u}", [P, 2 * PACK * (P // 2)], BF16) for u, kib in enumerate(kibs)]
+            for c, kibs in enumerate(LAST_BF_KIB)
+        ]
         words_all = [placed_at(kib, f"words_all{g}", [P, T], I32) for g, kib in enumerate(WORDS_ALL_KIB)]
-        w1_bf = [placed_at(kib, f"w1_bf{g}", [P, PACK * H], BF16) for g, kib in enumerate(W1_BF_KIB)]
+        w1_bf = [
+            [placed_at(kib, f"w1_bf{g}{u}", [P, LOWER * PACK * P], BF16) for u, kib in enumerate(kibs)]
+            for g, kibs in enumerate(W1_BF_KIB)
+        ]
         words = [placed_at(kib, f"words{g}", [P, S], U32) for g, kib in enumerate(WORDS_KIB)]
         scales = [placed_at(kib, f"scales{h}", [P, HALF], U8) for h, kib in enumerate(SCALES_KIB)]
         w2_raw = placed_at(W2_RAW_KIB, "w2_raw", [P, PACK, N], F32)
@@ -83,6 +96,31 @@ def tile_picked_pick_mlp_relu2_sub_p_kernel(tc, x_words, x_scales, w1, w2, offs,
             rows = w1[g * K_PASS : (g + 1) * K_PASS, :]
             nc.sync.dma_start(out=w1_raw[g][:], in_=rows.rearrange("(p j) c -> p j c", j=PACK))
 
+        def load_last(c):
+            rows = w1[LAST * K_PASS :, c * (H // 2) : (c + 1) * (H // 2)]
+            nc.sync.dma_start(out=last_raw[c][:], in_=rows.rearrange("(p j) c -> p j c", j=PACK))
+
+        def cast_last(c):
+            lower, upper = (last_bf[c][u][:].rearrange("p (t m j) -> p m j t", t=LOWER, j=PACK) for u in range(2))
+            src = last_raw[c][:].rearrange("p j (m t) -> p m j t", t=PACK)
+            if c == 0:
+                nc.scalar.activation(out=lower, in_=src[:, :, :, :LOWER], func=ACT.Copy)
+                nc.scalar.activation(out=upper, in_=src[:, :, :, LOWER:], func=ACT.Copy)
+            else:
+                split = LAST_SCALAR_COLUMNS
+                nc.scalar.activation(out=lower[:, :split], in_=src[:, :split, :, :LOWER], func=ACT.Copy)
+                nc.vector.tensor_copy(out=upper, in_=src[:, :, :, LOWER:])
+                nc.vector.tensor_copy(out=lower[:, split:], in_=src[:, split:, :, :LOWER])
+
+        def quantise_last(c, t):
+            columns = slice(t * P + c * (P // 2), t * P + (c + 1) * (P // 2))
+            u, e = divmod(t, LOWER)
+            nc.vector.quantize_mx(
+                out=w1_codes[LAST][:, columns].bitcast(FP8X4),
+                scales=w1_scales[LAST][:, columns],
+                in_=last_bf[c][u][:, e * 2 * P : (e + 1) * 2 * P],
+            )
+
         def list_slice(lo, hi):
             return offsets[:, lo // LIST_ROWS : hi // LIST_ROWS]
 
@@ -94,18 +132,18 @@ def tile_picked_pick_mlp_relu2_sub_p_kernel(tc, x_words, x_scales, w1, w2, offs,
             nc.vector.tensor_copy(scales[h][:], scales_all[:].bitcast(U8).indirect(entries))
 
         def cast_w1(g):
-            dst = w1_bf[g][:].rearrange("p (t m j) -> p m j t", t=PACK, j=PACK)
+            lower, upper = (w1_bf[g][u][:].rearrange("p (t m j) -> p m j t", t=LOWER, j=PACK) for u in range(2))
             src = w1_raw[g][:].rearrange("p j (m t) -> p m j t", t=PACK)
-            split = SCALAR_CAST_COLUMNS[g]
-            nc.scalar.activation(out=dst[:, :split, :, :LOWER], in_=src[:, :split, :, :LOWER], func=ACT.Copy)
-            nc.vector.tensor_copy(out=dst[:, :, :, LOWER:], in_=src[:, :, :, LOWER:])
-            nc.vector.tensor_copy(out=dst[:, split:, :, :LOWER], in_=src[:, split:, :, :LOWER])
+            split = SCALAR_UPPER_COLUMNS[g]
+            nc.scalar.activation(out=lower, in_=src[:, :, :, :LOWER], func=ACT.Copy)
+            if split:
+                nc.scalar.activation(out=upper[:, :split], in_=src[:, :split, :, LOWER:], func=ACT.Copy)
+            nc.vector.tensor_copy(out=upper[:, split:], in_=src[:, split:, :, LOWER:])
 
-        def quantise_w1(g, lo, hi):
+        def quantise_w1(g, u):
+            columns = slice(u * LOWER * P, (u + 1) * LOWER * P)
             nc.vector.quantize_mx(
-                out=w1_codes[g][:, lo:hi].bitcast(FP8X4),
-                scales=w1_scales[g][:, lo:hi],
-                in_=w1_bf[g][:, PACK * lo : PACK * hi],
+                out=w1_codes[g][:, columns].bitcast(FP8X4), scales=w1_scales[g][:, columns], in_=w1_bf[g][u][:]
             )
 
         def first_product(g):
@@ -135,25 +173,33 @@ def tile_picked_pick_mlp_relu2_sub_p_kernel(tc, x_words, x_scales, w1, w2, offs,
 
         gather_words(0, 0, S)
         load_w1(1)
-        load_w1(2)
+        load_last(0)
         gather_words(1, 0, S)
+        load_last(1)
         load_words(2)
         nc.sync.dma_start(out=w2_raw[:], in_=w2.rearrange("(p j) m -> p j m", j=PACK))
 
         cast_w1(0)
         gather_scales(0)
-        quantise_w1(0, 0, H)
         gather_scales(1)
+        quantise_w1(0, 1)
+        quantise_w1(0, 0)
         first_product(0)
 
         cast_w1(1)
-        quantise_w1(1, 0, H)
+        quantise_w1(1, 1)
+        quantise_w1(1, 0)
         first_product(1)
 
-        cast_w1(LAST)
-        quantise_w1(LAST, LOWER * P, H)
+        cast_last(0)
+        for t in range(LOWER):
+            quantise_last(0, t)
+        cast_last(1)
+        for t in range(LOWER, PACK):
+            quantise_last(0, t)
+        for t in TILE_ORDER:
+            quantise_last(1, t)
         gather_words(LAST, 0, HALF)
-        quantise_w1(LAST, 0, LOWER * P)
         gather_words(LAST, HALF, S)
         first_product(LAST)
 
@@ -167,7 +213,9 @@ def tile_picked_pick_mlp_relu2_sub_p_kernel(tc, x_words, x_scales, w1, w2, offs,
         h_bf = [kept(f"h_bf{q}", [P, PACK * CHUNK], BF16) for q in range(CHUNKS)]
         h_codes = [kept(f"h_codes{q}", [P, CHUNK], U32) for q in range(CHUNKS)]
         h_scales = [kept(f"h_scales{q}", [P, CHUNK], U8) for q in range(CHUNKS)]
-        y_sb = [keep.tile([P, CHUNK], F32, name=f"y_sb{q}") for q in range(CHUNKS)]
+        y_first = keep.tile([P, HALF], F32, name="y_first")
+        y_sb = [y_first[:, :CHUNK], y_first[:, CHUNK:]]
+        y_sb += [keep.tile([P, CHUNK], F32, name=f"y_sb{q}")[:] for q in range(2, CHUNKS)]
 
         def square_operands(q, lo, hi):
             h, first = divmod(q * CHUNK, HALF)
@@ -216,7 +264,10 @@ def tile_picked_pick_mlp_relu2_sub_p_kernel(tc, x_words, x_scales, w1, w2, offs,
                 stop=True,
             )
             if q < CHUNKS - 1:
-                nc.scalar.activation(out=y_sb[q][:], in_=y[:], func=ACT.Copy)
+                nc.scalar.activation(out=y_sb[q], in_=y[:], func=ACT.Copy)
             else:
-                nc.vector.tensor_copy(out=y_sb[q][:], in_=y[:])
-            nc.sync.dma_start(out=out[:, q * CHUNK : (q + 1) * CHUNK], in_=y_sb[q][:])
+                nc.vector.tensor_copy(out=y_sb[q], in_=y[:])
+            if q == 1:
+                nc.sync.dma_start(out=out[:, :HALF], in_=y_first[:])
+            elif q > 1:
+                nc.sync.dma_start(out=out[:, q * CHUNK : (q + 1) * CHUNK], in_=y_sb[q])

@@ -24,28 +24,23 @@ QUADRANT = 32
 SCALE_ROWS = 4
 LIST_ROWS = 16
 LINE = 4
-
-HALF = S // 2
+PAIRS = 2
+GROUPS = H // 16
 CHUNK = 128
 CHUNKS = S // CHUNK
+STORES = ((0, 256), (256, 384), (384, 512))
 
-LOWER = PACK // 2
-TILE_ORDER = (2, 3, 0, 1)
-SCALAR_UPPER_COLUMNS = (64, 0)
-LAST_SCALAR_COLUMNS = 48
-SCALAR_LAST_TOKENS = 40
+SCALAR_GROUPS = ((32, 16), (32, 0), (12, 12))
+SCALAR_LAST_TOKENS = 64
 
-W1_RAW_KIB = (26, 0)
-LAST_RAW_KIB = (10, 14)
-WORDS_ALL_KIB = (7, 17, 20)
-W1_BF_KIB = ((34, 36), (38, 36))
-W1_CODES_KIB = (52, 54, 56)
-SCALES_ALL_KIB = 53
-LAST_BF_KIB = ((64, 67), (65, 64))
-WORDS_KIB = (42, 44, 16)
-SCALES_KIB = (46, 47)
-W2_RAW_KIB = 18
-W2_BF_KIB = 14
+W1_RAW_KIB = (26, 0, 10)
+WORDS_ALL_KIB = (7, 64, 66)
+W1_BF_KIB = ((36, 38), (40, 38), (54, 56))
+W1_CODES_KIB = (48, 50, 52)
+SCALES_ALL_KIB = 48
+W2_RAW_KIB = 27
+W2_BF_KIB = 31.5
+POSITIVE_KIB = (26, 28, 30, 32)
 
 
 def tile_picked_pick_mlp_relu2_sub_p_kernel(tc, x_words, x_scales, w1, w2, offs, out):
@@ -62,32 +57,28 @@ def tile_picked_pick_mlp_relu2_sub_p_kernel(tc, x_words, x_scales, w1, w2, offs,
             return placed.tile(shape, dtype, name=name, tag=name, align_bytes=64, offset=int(1024 * kib))
 
         offsets = keep.tile([P, S // LIST_ROWS], U16, name="offsets")
-        w1_codes = [placed_at(kib, f"w1_codes{g}", [P, H], U32) for g, kib in enumerate(W1_CODES_KIB)]
-        w1_scales = [kept(f"w1_scales{g}", [P, H], U8) for g in range(PASSES)]
-        w2_codes = kept("w2_codes", [P, N], U32)
-        w2_scales = kept("w2_scales", [P, N], U8)
-
         scales_all = placed_at(SCALES_ALL_KIB, "scales_all", [P, T // 4], I32)
-        w1_raw = [placed_at(kib, f"w1_raw{g}", [P, PACK, H], F32) for g, kib in enumerate(W1_RAW_KIB)]
-        last_raw = [placed_at(kib, f"last_raw{c}", [P, PACK, H // 2], F32) for c, kib in enumerate(LAST_RAW_KIB)]
-        last_bf = [
-            [placed_at(kib, f"last_bf{c}{u}", [P, 2 * PACK * (P // 2)], BF16) for u, kib in enumerate(kibs)]
-            for c, kibs in enumerate(LAST_BF_KIB)
-        ]
         words_all = [placed_at(kib, f"words_all{g}", [P, T], I32) for g, kib in enumerate(WORDS_ALL_KIB)]
+        w1_raw = [placed_at(kib, f"w1_raw{g}", [P, PACK, H], F32) for g, kib in enumerate(W1_RAW_KIB)]
         w1_bf = [
-            [placed_at(kib, f"w1_bf{g}{u}", [P, LOWER * PACK * P], BF16) for u, kib in enumerate(kibs)]
+            [placed_at(kib, f"w1_bf{g}{u}", [P, PACK * H // PAIRS], BF16) for u, kib in enumerate(kibs)]
             for g, kibs in enumerate(W1_BF_KIB)
         ]
-        words = [placed_at(kib, f"words{g}", [P, S], U32) for g, kib in enumerate(WORDS_KIB)]
-        scales = [placed_at(kib, f"scales{h}", [P, HALF], U8) for h, kib in enumerate(SCALES_KIB)]
+        w1_codes = [placed_at(kib, f"w1_codes{g}", [P, H], U32) for g, kib in enumerate(W1_CODES_KIB)]
+        w1_scales = [kept(f"w1_scales{g}", [P, H], U8) for g in range(PASSES)]
+        words = [kept(f"words{g}", [P, S], U32) for g in range(PASSES)]
+        scales = kept("scales", [P, S], U8)
         w2_raw = placed_at(W2_RAW_KIB, "w2_raw", [P, PACK, N], F32)
         w2_bf = placed_at(W2_BF_KIB, "w2_bf", [P, PACK * N], BF16)
-
-        acc = [
-            [psum.tile([P, HALF], F32, name=f"acc{h}{t}", tag=f"bank{PACK * h + t}") for t in range(PACK)]
-            for h in range(2)
-        ]
+        w2_codes = kept("w2_codes", [P, N], U32)
+        w2_scales = kept("w2_scales", [P, N], U8)
+        positive = [placed_at(kib, f"positive{q}", [P, PACK * CHUNK], F32) for q, kib in enumerate(POSITIVE_KIB)]
+        h_bf = [kept(f"h_bf{q}", [P, PACK * CHUNK], BF16) for q in range(CHUNKS)]
+        h_codes = [kept(f"h_codes{q}", [P, CHUNK], U32) for q in range(CHUNKS)]
+        h_scales = [kept(f"h_scales{q}", [P, CHUNK], U8) for q in range(CHUNKS)]
+        y_sb = [kept(f"y_sb{r}", [P, hi - lo], F32) for r, (lo, hi) in enumerate(STORES)]
+        acc = [psum.tile([P, PACK, CHUNK], F32, name=f"acc{q}") for q in range(CHUNKS)]
+        y = [psum.tile([P, CHUNK], F32, name=f"y{q}") for q in range(CHUNKS)]
 
         def load_words(g):
             nc.sync.dma_start(out=words_all[g][:], in_=x_words[g].rearrange("p c r -> p (c r)").bitcast(I32))
@@ -96,166 +87,64 @@ def tile_picked_pick_mlp_relu2_sub_p_kernel(tc, x_words, x_scales, w1, w2, offs,
             rows = w1[g * K_PASS : (g + 1) * K_PASS, :]
             nc.sync.dma_start(out=w1_raw[g][:], in_=rows.rearrange("(p j) c -> p j c", j=PACK))
 
-        def load_last(c):
-            rows = w1[LAST * K_PASS :, c * (H // 2) : (c + 1) * (H // 2)]
-            nc.sync.dma_start(out=last_raw[c][:], in_=rows.rearrange("(p j) c -> p j c", j=PACK))
-
-        def cast_last(c):
-            lower, upper = (last_bf[c][u][:].rearrange("p (t m j) -> p m j t", t=LOWER, j=PACK) for u in range(2))
-            src = last_raw[c][:].rearrange("p j (m t) -> p m j t", t=PACK)
-            if c == 0:
-                nc.scalar.activation(out=lower, in_=src[:, :, :, :LOWER], func=ACT.Copy)
-                nc.scalar.activation(out=upper, in_=src[:, :, :, LOWER:], func=ACT.Copy)
-            else:
-                split = LAST_SCALAR_COLUMNS
-                nc.scalar.activation(out=lower[:, :split], in_=src[:, :split, :, :LOWER], func=ACT.Copy)
-                nc.vector.tensor_copy(out=upper, in_=src[:, :, :, LOWER:])
-                nc.vector.tensor_copy(out=lower[:, split:], in_=src[:, split:, :, :LOWER])
-
-        def quantise_last(c, t):
-            columns = slice(t * P + c * (P // 2), t * P + (c + 1) * (P // 2))
-            u, e = divmod(t, LOWER)
-            nc.vector.quantize_mx(
-                out=w1_codes[LAST][:, columns].bitcast(FP8X4),
-                scales=w1_scales[LAST][:, columns],
-                in_=last_bf[c][u][:, e * 2 * P : (e + 1) * 2 * P],
-            )
-
-        def list_slice(lo, hi):
-            return offsets[:, lo // LIST_ROWS : hi // LIST_ROWS]
-
         def gather_words(g, lo, hi):
-            nc.vector.tensor_copy(words[g][:, lo:hi], words_all[g][:].bitcast(U32).indirect(list_slice(lo, hi)))
+            entries = offsets[:, lo // LIST_ROWS : hi // LIST_ROWS]
+            nc.vector.tensor_copy(words[g][:, lo:hi], words_all[g][:].bitcast(U32).indirect(entries))
 
-        def gather_scales(h):
-            entries = list_slice(h * HALF, (h + 1) * HALF)
-            nc.vector.tensor_copy(scales[h][:], scales_all[:].bitcast(U8).indirect(entries))
-
-        def cast_w1(g):
-            lower, upper = (w1_bf[g][u][:].rearrange("p (t m j) -> p m j t", t=LOWER, j=PACK) for u in range(2))
-            src = w1_raw[g][:].rearrange("p j (m t) -> p m j t", t=PACK)
-            split = SCALAR_UPPER_COLUMNS[g]
-            nc.scalar.activation(out=lower, in_=src[:, :, :, :LOWER], func=ACT.Copy)
-            if split:
-                nc.scalar.activation(out=upper[:, :split], in_=src[:, :split, :, LOWER:], func=ACT.Copy)
-            nc.vector.tensor_copy(out=upper[:, split:], in_=src[:, split:, :, LOWER:])
+        def cast_w1(g, u):
+            dst = w1_bf[g][u][:].rearrange("p (e a c b j) -> p a c j b e", e=2, c=2, b=2, j=PACK)
+            src = w1_raw[g][:].rearrange("p j (a u c b e) -> p u a c j b e", u=PAIRS, c=2, b=2, e=2)[:, u]
+            split = SCALAR_GROUPS[g][u]
+            if split > 0:
+                nc.scalar.copy(out=dst[:, :split], in_=src[:, :split])
+            if split < GROUPS:
+                nc.vector.tensor_copy(out=dst[:, split:], in_=src[:, split:])
 
         def quantise_w1(g, u):
-            columns = slice(u * LOWER * P, (u + 1) * LOWER * P)
+            columns = slice(u * H // PAIRS, (u + 1) * H // PAIRS)
             nc.vector.quantize_mx(
                 out=w1_codes[g][:, columns].bitcast(FP8X4), scales=w1_scales[g][:, columns], in_=w1_bf[g][u][:]
             )
 
-        def first_product(g):
-            for h in range(2):
-                for t in TILE_ORDER:
-                    channels = slice(t * P, (t + 1) * P)
-                    nc.tensor.matmul_mx(
-                        out=acc[h][t][:],
-                        lhsT=w1_codes[g][:, channels].bitcast(FP8X4),
-                        lhsT_scale=w1_scales[g][:, channels],
-                        rhs=words[g][:, h * HALF : (h + 1) * HALF].bitcast(FP8X4),
-                        rhs_scale=scales[h][SCALE_ROWS * g : P, :],
-                        start=(g == 0),
-                        stop=(g == LAST),
-                    )
+        def first_product(g, q, u):
+            tokens = slice(q * CHUNK, (q + 1) * CHUNK)
+            for e in range(2):
+                t = 2 * u + e
+                channels = slice(t * P, (t + 1) * P)
+                nc.tensor.matmul_mx(
+                    out=acc[q][:, t, :],
+                    lhsT=w1_codes[g][:, channels].bitcast(FP8X4),
+                    lhsT_scale=w1_scales[g][:, channels],
+                    rhs=words[g][:, tokens].bitcast(FP8X4),
+                    rhs_scale=scales[SCALE_ROWS * g : P, tokens],
+                    start=(g == 0 and u == 1 and e == 0),
+                    stop=(g == LAST and u == 0 and e == 1),
+                )
 
-        nc.vector.memset(scales_all[:], 0)
-        load_words(0)
-        nc.sync.dma_start(offsets[:], offs)
-        load_words(1)
-        load_w1(0)
-        for q in range(P // QUADRANT):
-            nc.sync.dma_start(
-                out=scales_all[QUADRANT * q : QUADRANT * q + SCALE_ROWS * PASSES, :],
-                in_=x_scales[:, SCALE_ROWS * q : SCALE_ROWS * (q + 1), :].bitcast(I32),
-            )
+        def by_token(tile, lo=0, hi=CHUNK):
+            return tile[:, PACK * lo : PACK * hi].rearrange("p (n t) -> p n t", t=PACK)
 
-        gather_words(0, 0, S)
-        load_w1(1)
-        load_last(0)
-        gather_words(1, 0, S)
-        load_last(1)
-        load_words(2)
-        nc.sync.dma_start(out=w2_raw[:], in_=w2.rearrange("(p j) m -> p j m", j=PACK))
-
-        cast_w1(0)
-        gather_scales(0)
-        gather_scales(1)
-        quantise_w1(0, 1)
-        quantise_w1(0, 0)
-        first_product(0)
-
-        cast_w1(1)
-        quantise_w1(1, 1)
-        quantise_w1(1, 0)
-        first_product(1)
-
-        cast_last(0)
-        for t in range(LOWER):
-            quantise_last(0, t)
-        cast_last(1)
-        for t in range(LOWER, PACK):
-            quantise_last(0, t)
-        for t in TILE_ORDER:
-            quantise_last(1, t)
-        gather_words(LAST, 0, HALF)
-        gather_words(LAST, HALF, S)
-        first_product(LAST)
-
-        nc.scalar.activation(
-            out=w2_bf[:].rearrange("p (c e j) -> p c j e", e=LINE, j=PACK),
-            in_=w2_raw[:].rearrange("p j (c e) -> p c j e", e=LINE),
-            func=ACT.Copy,
-        )
-
-        positive = [keep.tile([P, PACK, HALF], F32, name=f"positive{h}") for h in range(2)]
-        h_bf = [kept(f"h_bf{q}", [P, PACK * CHUNK], BF16) for q in range(CHUNKS)]
-        h_codes = [kept(f"h_codes{q}", [P, CHUNK], U32) for q in range(CHUNKS)]
-        h_scales = [kept(f"h_scales{q}", [P, CHUNK], U8) for q in range(CHUNKS)]
-        y_first = keep.tile([P, HALF], F32, name="y_first")
-        y_sb = [y_first[:, :CHUNK], y_first[:, CHUNK:]]
-        y_sb += [keep.tile([P, CHUNK], F32, name=f"y_sb{q}")[:] for q in range(2, CHUNKS)]
-
-        def square_operands(q, lo, hi):
-            h, first = divmod(q * CHUNK, HALF)
-            src = positive[h][:, :, first + lo : first + hi].rearrange("p t (c e) -> p c t e", e=LINE)
-            dst = h_bf[q][:, PACK * lo : PACK * hi].rearrange("p (c e t) -> p c t e", e=LINE, t=PACK)
-            return dst, src
+        def relu(q, on_scalar):
+            sums = acc[q][:].rearrange("p t n -> p n t")
+            if on_scalar:
+                nc.scalar.activation(out=by_token(positive[q]), in_=sums, func=ACT.Relu)
+            else:
+                nc.vector.tensor_scalar_max(by_token(positive[q]), sums, 0.0)
 
         def square_on_scalar(q, lo, hi):
-            dst, src = square_operands(q, lo, hi)
-            nc.scalar.activation(out=dst, in_=src, func=ACT.Square)
+            columns = slice(PACK * lo, PACK * hi)
+            nc.scalar.activation(out=h_bf[q][:, columns], in_=positive[q][:, columns], func=ACT.Square)
 
         def square_on_vector(q, lo, hi):
-            dst, src = square_operands(q, lo, hi)
-            nc.vector.tensor_tensor(dst, src, src, ALU.mult)
+            columns = slice(PACK * lo, PACK * hi)
+            nc.vector.tensor_tensor(h_bf[q][:, columns], positive[q][:, columns], positive[q][:, columns], ALU.mult)
 
         def quantise_h(q):
             nc.vector.quantize_mx(out=h_codes[q][:].bitcast(FP8X4), scales=h_scales[q][:], in_=h_bf[q][:])
 
-        for h in range(2):
-            for t in TILE_ORDER:
-                if (h + t) % 2 == 0:
-                    nc.scalar.activation(out=positive[h][:, t, :], in_=acc[h][t][:], func=ACT.Relu)
-                else:
-                    nc.vector.tensor_scalar_max(positive[h][:, t, :], acc[h][t][:], 0.0)
-        nc.vector.quantize_mx(out=w2_codes[:].bitcast(FP8X4), scales=w2_scales[:], in_=w2_bf[:])
-
-        square_on_scalar(0, 0, CHUNK)
-        square_on_vector(1, 0, CHUNK)
-        square_on_scalar(2, 0, CHUNK)
-        square_on_vector(3, SCALAR_LAST_TOKENS, CHUNK)
-        quantise_h(0)
-        quantise_h(1)
-        square_on_scalar(3, 0, SCALAR_LAST_TOKENS)
-        quantise_h(2)
-        quantise_h(3)
-
-        for q in range(CHUNKS):
-            y = psum.tile([P, CHUNK], F32, name=f"y{q}", tag=f"bank{q}")
+        def second_product(q):
             nc.tensor.matmul_mx(
-                out=y[:],
+                out=y[q][:],
                 lhsT=w2_codes[:].bitcast(FP8X4),
                 lhsT_scale=w2_scales[:],
                 rhs=h_codes[q][:].bitcast(FP8X4),
@@ -263,11 +152,76 @@ def tile_picked_pick_mlp_relu2_sub_p_kernel(tc, x_words, x_scales, w1, w2, offs,
                 start=True,
                 stop=True,
             )
-            if q < CHUNKS - 1:
-                nc.scalar.activation(out=y_sb[q], in_=y[:], func=ACT.Copy)
+
+        def store(q, on_scalar):
+            r = min(r for r, (lo, hi) in enumerate(STORES) if (q + 1) * CHUNK <= hi)
+            lo, hi = STORES[r]
+            dst = y_sb[r][:, q * CHUNK - lo : (q + 1) * CHUNK - lo]
+            if on_scalar:
+                nc.scalar.activation(out=dst, in_=y[q][:], func=ACT.Copy)
             else:
-                nc.vector.tensor_copy(out=y_sb[q], in_=y[:])
-            if q == 1:
-                nc.sync.dma_start(out=out[:, :HALF], in_=y_first[:])
-            elif q > 1:
-                nc.sync.dma_start(out=out[:, q * CHUNK : (q + 1) * CHUNK], in_=y_sb[q])
+                nc.vector.tensor_copy(out=dst, in_=y[q][:])
+            if (q + 1) * CHUNK == hi:
+                nc.sync.dma_start(out=out[:, lo:hi], in_=y_sb[r][:])
+
+        nc.vector.memset(scales_all[:], 0)
+        load_words(0)
+        nc.sync.dma_start(offsets[:], offs)
+        load_words(1)
+        load_w1(0)
+        for b in range(P // QUADRANT):
+            nc.sync.dma_start(
+                out=scales_all[QUADRANT * b : QUADRANT * b + SCALE_ROWS * PASSES, :],
+                in_=x_scales[:, SCALE_ROWS * b : SCALE_ROWS * (b + 1), :].bitcast(I32),
+            )
+        gather_words(0, 0, S)
+        load_w1(1)
+        load_w1(2)
+        gather_words(1, 0, S)
+        load_words(2)
+
+        for g in range(LAST):
+            for u in (1, 0):
+                cast_w1(g, u)
+            if g == 0:
+                w2_rows = w2.rearrange("(a u l e) m -> u a l (e m)", u=PAIRS, l=4, e=2)
+                for u in range(PAIRS):
+                    nc.sync.dma_start(out=w2_raw[:, 2 * u : 2 * u + 2, :].rearrange("p e m -> p (e m)"), in_=w2_rows[u])
+                nc.vector.tensor_copy(scales[:], scales_all[:].bitcast(U8).indirect(offsets[:]))
+            for u in (1, 0):
+                quantise_w1(g, u)
+                for q in range(CHUNKS):
+                    first_product(g, q, u)
+
+        for u in (1, 0):
+            cast_w1(LAST, u)
+        for u in (1, 0):
+            quantise_w1(LAST, u)
+        for q in range(CHUNKS):
+            gather_words(LAST, q * CHUNK, (q + 1) * CHUNK)
+            for u in (1, 0):
+                first_product(LAST, q, u)
+
+        nc.scalar.activation(
+            out=w2_bf[:].rearrange("p (c l j) -> p c j l", l=LINE, j=PACK),
+            in_=w2_raw[:].rearrange("p j (c l) -> p c j l", l=LINE),
+            func=ACT.Copy,
+        )
+        nc.vector.quantize_mx(out=w2_codes[:].bitcast(FP8X4), scales=w2_scales[:], in_=w2_bf[:])
+
+        relu(0, True)
+        relu(1, False)
+        relu(2, True)
+        relu(3, False)
+        square_on_scalar(0, 0, CHUNK)
+        square_on_vector(1, 0, CHUNK)
+        square_on_scalar(2, 0, CHUNK)
+        quantise_h(0)
+        quantise_h(1)
+        square_on_scalar(3, 0, SCALAR_LAST_TOKENS)
+        square_on_vector(3, SCALAR_LAST_TOKENS, CHUNK)
+        quantise_h(2)
+        quantise_h(3)
+        for q in range(CHUNKS):
+            second_product(q)
+            store(q, q < CHUNKS - 1)

@@ -30,17 +30,17 @@ CHUNK = 128
 CHUNKS = S // CHUNK
 STORES = ((0, 256), (256, 384), (384, 512))
 
-SCALAR_GROUPS = ((32, 16), (32, 0), (12, 12))
-SCALAR_LAST_TOKENS = 64
+SCALAR_GROUPS = ((32, 16), (32, 0), (10, 12))
+SCALAR_LAST_TOKENS = 96
 
 W1_RAW_KIB = (26, 0, 10)
 WORDS_ALL_KIB = (7, 64, 66)
 W1_BF_KIB = ((36, 38), (40, 38), (54, 56))
 W1_CODES_KIB = (48, 50, 52)
 SCALES_ALL_KIB = 48
-W2_RAW_KIB = 27
-W2_BF_KIB = 31.5
-POSITIVE_KIB = (26, 28, 30, 32)
+W2_RAW_KIB = 1
+W2_BF_KIB = 5.5
+POSITIVE_KIB = (0, 2, 4, 6)
 
 
 def tile_picked_pick_mlp_relu2_sub_p_kernel(tc, x_words, x_scales, w1, w2, offs, out):
@@ -136,8 +136,10 @@ def tile_picked_pick_mlp_relu2_sub_p_kernel(tc, x_words, x_scales, w1, w2, offs,
             nc.scalar.activation(out=h_bf[q][:, columns], in_=positive[q][:, columns], func=ACT.Square)
 
         def square_on_vector(q, lo, hi):
-            columns = slice(PACK * lo, PACK * hi)
-            nc.vector.tensor_tensor(h_bf[q][:, columns], positive[q][:, columns], positive[q][:, columns], ALU.mult)
+            sums = acc[q][:, :, lo:hi].rearrange("p t n -> p n t")
+            nc.vector.scalar_tensor_tensor(
+                by_token(h_bf[q], lo, hi), sums, 0.0, by_token(positive[q], lo, hi), ALU.max, ALU.mult
+            )
 
         def quantise_h(q):
             nc.vector.quantize_mx(out=h_codes[q][:].bitcast(FP8X4), scales=h_scales[q][:], in_=h_bf[q][:])
@@ -184,10 +186,11 @@ def tile_picked_pick_mlp_relu2_sub_p_kernel(tc, x_words, x_scales, w1, w2, offs,
             for u in (1, 0):
                 cast_w1(g, u)
             if g == 0:
+                nc.vector.tensor_copy(scales[:], scales_all[:].bitcast(U8).indirect(offsets[:]))
+            else:
                 w2_rows = w2.rearrange("(a u l e) m -> u a l (e m)", u=PAIRS, l=4, e=2)
                 for u in range(PAIRS):
                     nc.sync.dma_start(out=w2_raw[:, 2 * u : 2 * u + 2, :].rearrange("p e m -> p (e m)"), in_=w2_rows[u])
-                nc.vector.tensor_copy(scales[:], scales_all[:].bitcast(U8).indirect(offsets[:]))
             for u in (1, 0):
                 quantise_w1(g, u)
                 for q in range(CHUNKS):
@@ -211,9 +214,11 @@ def tile_picked_pick_mlp_relu2_sub_p_kernel(tc, x_words, x_scales, w1, w2, offs,
 
         relu(0, True)
         relu(1, False)
+        shared = slice(0, PACK * 64)
+        nc.gpsimd.tensor_tensor(h_bf[0][:, shared], positive[0][:, shared], positive[0][:, shared], ALU.mult)
         relu(2, True)
         relu(3, False)
-        square_on_scalar(0, 0, CHUNK)
+        square_on_scalar(0, 64, CHUNK)
         square_on_vector(1, 0, CHUNK)
         square_on_scalar(2, 0, CHUNK)
         quantise_h(0)

@@ -25,13 +25,17 @@ SCALE_ROWS = 4
 LIST_ROWS = 16
 LINE = 4
 PAIRS = 2
+PAIR_ORDER = (1, 0)
 GROUPS = H // 16
-CHUNK = 128
-CHUNKS = S // CHUNK
+QUARTER = 128
+QUARTERS = S // QUARTER
 STORES = ((0, 256), (256, 384), (384, 512))
 
 SCALAR_GROUPS = ((32, 16), (32, 0), (10, 12))
-SCALAR_LAST_TOKENS = 96
+GPSIMD_TOKENS = 96
+SCALAR_SECOND_TOKENS = 32
+SCALAR_LAST_TOKENS = 80
+QUANTISE_ORDER = (1, 0, 2, 3)
 
 W1_RAW_KIB = (26, 0, 10)
 WORDS_ALL_KIB = (7, 64, 66)
@@ -72,13 +76,13 @@ def tile_picked_pick_mlp_relu2_sub_p_kernel(tc, x_words, x_scales, w1, w2, offs,
         w2_bf = placed_at(W2_BF_KIB, "w2_bf", [P, PACK * N], BF16)
         w2_codes = kept("w2_codes", [P, N], U32)
         w2_scales = kept("w2_scales", [P, N], U8)
-        positive = [placed_at(kib, f"positive{q}", [P, PACK * CHUNK], F32) for q, kib in enumerate(POSITIVE_KIB)]
-        h_bf = [kept(f"h_bf{q}", [P, PACK * CHUNK], BF16) for q in range(CHUNKS)]
-        h_codes = [kept(f"h_codes{q}", [P, CHUNK], U32) for q in range(CHUNKS)]
-        h_scales = [kept(f"h_scales{q}", [P, CHUNK], U8) for q in range(CHUNKS)]
+        positive = [placed_at(kib, f"positive{q}", [P, PACK * QUARTER], F32) for q, kib in enumerate(POSITIVE_KIB)]
+        h_bf = [kept(f"h_bf{q}", [P, PACK * QUARTER], BF16) for q in range(QUARTERS)]
+        h_codes = [kept(f"h_codes{q}", [P, QUARTER], U32) for q in range(QUARTERS)]
+        h_scales = [kept(f"h_scales{q}", [P, QUARTER], U8) for q in range(QUARTERS)]
         y_sb = [kept(f"y_sb{r}", [P, hi - lo], F32) for r, (lo, hi) in enumerate(STORES)]
-        acc = [psum.tile([P, PACK, CHUNK], F32, name=f"acc{q}") for q in range(CHUNKS)]
-        y = [psum.tile([P, CHUNK], F32, name=f"y{q}") for q in range(CHUNKS)]
+        acc = [psum.tile([P, PACK, QUARTER], F32, name=f"acc{q}") for q in range(QUARTERS)]
+        y = [psum.tile([P, QUARTER], F32, name=f"y{q}") for q in range(QUARTERS)]
 
         def load_words(g):
             nc.sync.dma_start(out=words_all[g][:], in_=x_words[g].rearrange("p c r -> p (c r)").bitcast(I32))
@@ -86,6 +90,11 @@ def tile_picked_pick_mlp_relu2_sub_p_kernel(tc, x_words, x_scales, w1, w2, offs,
         def load_w1(g):
             rows = w1[g * K_PASS : (g + 1) * K_PASS, :]
             nc.sync.dma_start(out=w1_raw[g][:], in_=rows.rearrange("(p j) c -> p j c", j=PACK))
+
+        def load_w2():
+            rows = w2.rearrange("(a u l e) m -> u a l (e m)", u=PAIRS, l=4, e=2)
+            for u in range(PAIRS):
+                nc.sync.dma_start(out=w2_raw[:, 2 * u : 2 * u + 2, :].rearrange("p e m -> p (e m)"), in_=rows[u])
 
         def gather_words(g, lo, hi):
             entries = offsets[:, lo // LIST_ROWS : hi // LIST_ROWS]
@@ -107,7 +116,7 @@ def tile_picked_pick_mlp_relu2_sub_p_kernel(tc, x_words, x_scales, w1, w2, offs,
             )
 
         def first_product(g, q, u):
-            tokens = slice(q * CHUNK, (q + 1) * CHUNK)
+            tokens = slice(q * QUARTER, (q + 1) * QUARTER)
             for e in range(2):
                 t = 2 * u + e
                 channels = slice(t * P, (t + 1) * P)
@@ -117,32 +126,39 @@ def tile_picked_pick_mlp_relu2_sub_p_kernel(tc, x_words, x_scales, w1, w2, offs,
                     lhsT_scale=w1_scales[g][:, channels],
                     rhs=words[g][:, tokens].bitcast(FP8X4),
                     rhs_scale=scales[SCALE_ROWS * g : P, tokens],
-                    start=(g == 0 and u == 1 and e == 0),
-                    stop=(g == LAST and u == 0 and e == 1),
+                    start=(g == 0 and u == PAIR_ORDER[0] and e == 0),
+                    stop=(g == LAST and u == PAIR_ORDER[-1] and e == 1),
                 )
 
-        def by_token(tile, lo=0, hi=CHUNK):
+        def sums_by_token(q, lo, hi):
+            return acc[q][:, :, lo:hi].rearrange("p t n -> p n t")
+
+        def by_token(tile, lo, hi):
             return tile[:, PACK * lo : PACK * hi].rearrange("p (n t) -> p n t", t=PACK)
 
-        def relu(q, on_scalar):
-            sums = acc[q][:].rearrange("p t n -> p n t")
-            if on_scalar:
-                nc.scalar.activation(out=by_token(positive[q]), in_=sums, func=ACT.Relu)
-            else:
-                nc.vector.tensor_scalar_max(by_token(positive[q]), sums, 0.0)
+        def relu_on_scalar(q):
+            nc.scalar.activation(out=by_token(positive[q], 0, QUARTER), in_=sums_by_token(q, 0, QUARTER), func=ACT.Relu)
+
+        def relu_on_vector(q):
+            nc.vector.tensor_scalar_max(by_token(positive[q], 0, QUARTER), sums_by_token(q, 0, QUARTER), 0.0)
+
+        def square_on_gpsimd(q, lo, hi):
+            columns = slice(PACK * lo, PACK * hi)
+            nc.gpsimd.tensor_tensor(h_bf[q][:, columns], positive[q][:, columns], positive[q][:, columns], ALU.mult)
 
         def square_on_scalar(q, lo, hi):
             columns = slice(PACK * lo, PACK * hi)
             nc.scalar.activation(out=h_bf[q][:, columns], in_=positive[q][:, columns], func=ACT.Square)
 
         def square_on_vector(q, lo, hi):
-            sums = acc[q][:, :, lo:hi].rearrange("p t n -> p n t")
             nc.vector.scalar_tensor_tensor(
-                by_token(h_bf[q], lo, hi), sums, 0.0, by_token(positive[q], lo, hi), ALU.max, ALU.mult
+                by_token(h_bf[q], lo, hi),
+                sums_by_token(q, lo, hi),
+                0.0,
+                by_token(positive[q], lo, hi),
+                ALU.max,
+                ALU.mult,
             )
-
-        def quantise_h(q):
-            nc.vector.quantize_mx(out=h_codes[q][:].bitcast(FP8X4), scales=h_scales[q][:], in_=h_bf[q][:])
 
         def second_product(q):
             nc.tensor.matmul_mx(
@@ -155,15 +171,15 @@ def tile_picked_pick_mlp_relu2_sub_p_kernel(tc, x_words, x_scales, w1, w2, offs,
                 stop=True,
             )
 
-        def store(q, on_scalar):
-            r = min(r for r, (lo, hi) in enumerate(STORES) if (q + 1) * CHUNK <= hi)
+        def store(q):
+            r = min(r for r, (lo, hi) in enumerate(STORES) if (q + 1) * QUARTER <= hi)
             lo, hi = STORES[r]
-            dst = y_sb[r][:, q * CHUNK - lo : (q + 1) * CHUNK - lo]
-            if on_scalar:
+            dst = y_sb[r][:, q * QUARTER - lo : (q + 1) * QUARTER - lo]
+            if q < QUARTERS - 1:
                 nc.scalar.activation(out=dst, in_=y[q][:], func=ACT.Copy)
             else:
                 nc.vector.tensor_copy(out=dst, in_=y[q][:])
-            if (q + 1) * CHUNK == hi:
+            if (q + 1) * QUARTER == hi:
                 nc.sync.dma_start(out=out[:, lo:hi], in_=y_sb[r][:])
 
         nc.vector.memset(scales_all[:], 0)
@@ -178,55 +194,51 @@ def tile_picked_pick_mlp_relu2_sub_p_kernel(tc, x_words, x_scales, w1, w2, offs,
             )
         gather_words(0, 0, S)
         load_w1(1)
-        load_w1(2)
+        load_w1(LAST)
         gather_words(1, 0, S)
-        load_words(2)
+        load_words(LAST)
 
         for g in range(LAST):
-            for u in (1, 0):
+            for u in PAIR_ORDER:
                 cast_w1(g, u)
             if g == 0:
                 nc.vector.tensor_copy(scales[:], scales_all[:].bitcast(U8).indirect(offsets[:]))
             else:
-                w2_rows = w2.rearrange("(a u l e) m -> u a l (e m)", u=PAIRS, l=4, e=2)
-                for u in range(PAIRS):
-                    nc.sync.dma_start(out=w2_raw[:, 2 * u : 2 * u + 2, :].rearrange("p e m -> p (e m)"), in_=w2_rows[u])
-            for u in (1, 0):
+                load_w2()
+            for u in PAIR_ORDER:
                 quantise_w1(g, u)
-                for q in range(CHUNKS):
+                for q in range(QUARTERS):
                     first_product(g, q, u)
 
-        for u in (1, 0):
+        for u in PAIR_ORDER:
             cast_w1(LAST, u)
-        for u in (1, 0):
+        for u in PAIR_ORDER:
             quantise_w1(LAST, u)
-        for q in range(CHUNKS):
-            gather_words(LAST, q * CHUNK, (q + 1) * CHUNK)
-            for u in (1, 0):
+        for q in range(QUARTERS):
+            gather_words(LAST, q * QUARTER, (q + 1) * QUARTER)
+            for u in PAIR_ORDER:
                 first_product(LAST, q, u)
 
         nc.scalar.activation(
-            out=w2_bf[:].rearrange("p (c l j) -> p c j l", l=LINE, j=PACK),
-            in_=w2_raw[:].rearrange("p j (c l) -> p c j l", l=LINE),
+            out=w2_bf[:].rearrange("p (c v j) -> p c j v", v=LINE, j=PACK),
+            in_=w2_raw[:].rearrange("p j (c v) -> p c j v", v=LINE),
             func=ACT.Copy,
         )
         nc.vector.quantize_mx(out=w2_codes[:].bitcast(FP8X4), scales=w2_scales[:], in_=w2_bf[:])
 
-        relu(0, True)
-        relu(1, False)
-        shared = slice(0, PACK * 64)
-        nc.gpsimd.tensor_tensor(h_bf[0][:, shared], positive[0][:, shared], positive[0][:, shared], ALU.mult)
-        relu(2, True)
-        relu(3, False)
-        square_on_scalar(0, 64, CHUNK)
-        square_on_vector(1, 0, CHUNK)
-        square_on_scalar(2, 0, CHUNK)
-        quantise_h(0)
-        quantise_h(1)
+        relu_on_scalar(0)
+        relu_on_vector(1)
+        square_on_gpsimd(0, 0, GPSIMD_TOKENS)
+        relu_on_scalar(2)
+        relu_on_vector(3)
+        square_on_scalar(0, GPSIMD_TOKENS, QUARTER)
+        square_on_scalar(1, 0, SCALAR_SECOND_TOKENS)
+        square_on_vector(1, SCALAR_SECOND_TOKENS, QUARTER)
+        square_on_scalar(2, 0, QUARTER)
         square_on_scalar(3, 0, SCALAR_LAST_TOKENS)
-        square_on_vector(3, SCALAR_LAST_TOKENS, CHUNK)
-        quantise_h(2)
-        quantise_h(3)
-        for q in range(CHUNKS):
+        square_on_vector(3, SCALAR_LAST_TOKENS, QUARTER)
+        for q in QUANTISE_ORDER:
+            nc.vector.quantize_mx(out=h_codes[q][:].bitcast(FP8X4), scales=h_scales[q][:], in_=h_bf[q][:])
+        for q in range(QUARTERS):
             second_product(q)
-            store(q, q < CHUNKS - 1)
+            store(q)

@@ -29,19 +29,19 @@ PAIR_ORDER = (1, 0)
 GROUPS = H // 16
 QUARTER = 128
 QUARTERS = S // QUARTER
+UPPER, LOWER = PAIR_ORDER
 STORES = ((0, 256), (256, 384), (384, 512))
 
-SCALAR_GROUPS = ((32, 16), (32, 0), (10, 12))
+SCALAR_GROUPS = ((32, 16), (26, 0))
+SCALAR_GROUPS_LAST = ((0, 32), (10, 10))
 GPSIMD_TOKENS = 96
 SCALAR_SECOND_TOKENS = 32
 SCALAR_LAST_TOKENS = 80
 QUANTISE_ORDER = (1, 0, 2, 3)
 
-W1_RAW_KIB = (26, 0, 10)
-WORDS_ALL_KIB = (7, 64, 66)
-W1_BF_KIB = ((36, 38), (40, 38), (54, 56))
-W1_CODES_KIB = (48, 50, 52)
-SCALES_ALL_KIB = 48
+SCALES_ALL_KIB = 16
+W1_CODES_0_KIB = (16.5, 15.5)
+W1_BF_UPPER_KIB = 20
 W2_RAW_KIB = 1
 W2_BF_KIB = 5.5
 POSITIVE_KIB = (0, 2, 4, 6)
@@ -62,14 +62,24 @@ def tile_picked_pick_mlp_relu2_sub_p_kernel(tc, x_words, x_scales, w1, w2, offs,
 
         offsets = keep.tile([P, S // LIST_ROWS], U16, name="offsets")
         scales_all = placed_at(SCALES_ALL_KIB, "scales_all", [P, T // 4], I32)
-        words_all = [placed_at(kib, f"words_all{g}", [P, T], I32) for g, kib in enumerate(WORDS_ALL_KIB)]
-        w1_raw = [placed_at(kib, f"w1_raw{g}", [P, PACK, H], F32) for g, kib in enumerate(W1_RAW_KIB)]
+        words_early = kept("words_early", [P, LAST * T], I32)
+        words_last = kept("words_last", [P, T], I32)
+        words_all = [words_early[:, g * T : (g + 1) * T] for g in range(LAST)] + [words_last[:]]
+        w1_raw = [kept(f"w1_raw{g}", [P, PACK, H], F32) for g in range(LAST)]
+        w1_raw_last = [kept(f"w1_raw_last{d}", [P, 2, H], F32) for d in range(2)]
         w1_bf = [
-            [placed_at(kib, f"w1_bf{g}{u}", [P, PACK * H // PAIRS], BF16) for u, kib in enumerate(kibs)]
-            for g, kibs in enumerate(W1_BF_KIB)
+            [
+                placed_at(W1_BF_UPPER_KIB, f"w1_bf{g}{u}", [P, PACK * H // PAIRS], BF16)
+                if u == UPPER and g < LAST
+                else kept(f"w1_bf{g}{u}", [P, PACK * H // PAIRS], BF16)
+                for u in range(PAIRS)
+            ]
+            for g in range(PASSES)
         ]
-        w1_codes = [placed_at(kib, f"w1_codes{g}", [P, H], U32) for g, kib in enumerate(W1_CODES_KIB)]
-        w1_scales = [kept(f"w1_scales{g}", [P, H], U8) for g in range(PASSES)]
+        w1_codes = [[placed_at(kib, f"w1_codes0{u}", [P, H // PAIRS], U32) for u, kib in enumerate(W1_CODES_0_KIB)]] + [
+            [kept(f"w1_codes{g}{u}", [P, H // PAIRS], U32) for u in range(PAIRS)] for g in range(1, PASSES)
+        ]
+        w1_scales = [[kept(f"w1_scales{g}{u}", [P, H // PAIRS], U8) for u in range(PAIRS)] for g in range(PASSES)]
         words = [kept(f"words{g}", [P, S], U32) for g in range(PASSES)]
         scales = kept("scales", [P, S], U8)
         w2_raw = placed_at(W2_RAW_KIB, "w2_raw", [P, PACK, N], F32)
@@ -84,8 +94,9 @@ def tile_picked_pick_mlp_relu2_sub_p_kernel(tc, x_words, x_scales, w1, w2, offs,
         acc = [psum.tile([P, PACK, QUARTER], F32, name=f"acc{q}") for q in range(QUARTERS)]
         y = [psum.tile([P, QUARTER], F32, name=f"y{q}") for q in range(QUARTERS)]
 
-        def load_words(g):
-            nc.sync.dma_start(out=words_all[g][:], in_=x_words[g].rearrange("p c r -> p (c r)").bitcast(I32))
+        def load_w1_last(d):
+            rows = w1[LAST * K_PASS :, :].rearrange("(p j) c -> p j c", j=PACK)
+            nc.sync.dma_start(out=w1_raw_last[d][:], in_=rows[:, 2 * d : 2 * d + 2, :])
 
         def load_w1(g):
             rows = w1[g * K_PASS : (g + 1) * K_PASS, :]
@@ -98,32 +109,27 @@ def tile_picked_pick_mlp_relu2_sub_p_kernel(tc, x_words, x_scales, w1, w2, offs,
 
         def gather_words(g, lo, hi):
             entries = offsets[:, lo // LIST_ROWS : hi // LIST_ROWS]
-            nc.vector.tensor_copy(words[g][:, lo:hi], words_all[g][:].bitcast(U32).indirect(entries))
+            nc.vector.tensor_copy(words[g][:, lo:hi], words_all[g].bitcast(U32).indirect(entries))
 
-        def cast_w1(g, u):
-            dst = w1_bf[g][u][:].rearrange("p (e a c b j) -> p a c j b e", e=2, c=2, b=2, j=PACK)
-            src = w1_raw[g][:].rearrange("p j (a u c b e) -> p u a c j b e", u=PAIRS, c=2, b=2, e=2)[:, u]
-            split = SCALAR_GROUPS[g][u]
+        def cast_w1(g, u, raw, rows, split):
+            dst = w1_bf[g][u][:].rearrange("p (e a c b j) -> p a c j b e", e=2, c=2, b=2, j=PACK)[:, :, :, rows]
+            src = raw[:].rearrange("p j (a u c b e) -> p u a c j b e", u=PAIRS, c=2, b=2, e=2)[:, u]
             if split > 0:
                 nc.scalar.copy(out=dst[:, :split], in_=src[:, :split])
             if split < GROUPS:
                 nc.vector.tensor_copy(out=dst[:, split:], in_=src[:, split:])
 
         def quantise_w1(g, u):
-            columns = slice(u * H // PAIRS, (u + 1) * H // PAIRS)
-            nc.vector.quantize_mx(
-                out=w1_codes[g][:, columns].bitcast(FP8X4), scales=w1_scales[g][:, columns], in_=w1_bf[g][u][:]
-            )
+            nc.vector.quantize_mx(out=w1_codes[g][u][:].bitcast(FP8X4), scales=w1_scales[g][u][:], in_=w1_bf[g][u][:])
 
         def first_product(g, q, u):
             tokens = slice(q * QUARTER, (q + 1) * QUARTER)
             for e in range(2):
-                t = 2 * u + e
-                channels = slice(t * P, (t + 1) * P)
+                channels = slice(e * P, (e + 1) * P)
                 nc.tensor.matmul_mx(
-                    out=acc[q][:, t, :],
-                    lhsT=w1_codes[g][:, channels].bitcast(FP8X4),
-                    lhsT_scale=w1_scales[g][:, channels],
+                    out=acc[q][:, 2 * u + e, :],
+                    lhsT=w1_codes[g][u][:, channels].bitcast(FP8X4),
+                    lhsT_scale=w1_scales[g][u][:, channels],
                     rhs=words[g][:, tokens].bitcast(FP8X4),
                     rhs_scale=scales[SCALE_ROWS * g : P, tokens],
                     start=(g == 0 and u == PAIR_ORDER[0] and e == 0),
@@ -182,36 +188,39 @@ def tile_picked_pick_mlp_relu2_sub_p_kernel(tc, x_words, x_scales, w1, w2, offs,
             if (q + 1) * QUARTER == hi:
                 nc.sync.dma_start(out=out[:, lo:hi], in_=y_sb[r][:])
 
-        nc.vector.memset(scales_all[:], 0)
-        load_words(0)
+        nc.gpsimd.memset(scales_all[:], 0)
+        nc.sync.dma_start(
+            out=words_early[:].rearrange("p (g c) -> p g c", g=LAST),
+            in_=x_words[:LAST].rearrange("g p c r -> p g (c r)").bitcast(I32),
+        )
         nc.sync.dma_start(offsets[:], offs)
-        load_words(1)
         load_w1(0)
         for b in range(P // QUADRANT):
             nc.sync.dma_start(
                 out=scales_all[QUADRANT * b : QUADRANT * b + SCALE_ROWS * PASSES, :],
                 in_=x_scales[:, SCALE_ROWS * b : SCALE_ROWS * (b + 1), :].bitcast(I32),
             )
-        gather_words(0, 0, S)
         load_w1(1)
-        load_w1(LAST)
-        gather_words(1, 0, S)
-        load_words(LAST)
+        for d in range(2):
+            load_w1_last(d)
+        nc.sync.dma_start(out=words_last[:], in_=x_words[LAST].rearrange("p c r -> p (c r)").bitcast(I32))
+        load_w2()
 
         for g in range(LAST):
+            gather_words(g, 0, S)
+        for g in range(LAST):
             for u in PAIR_ORDER:
-                cast_w1(g, u)
+                cast_w1(g, u, w1_raw[g], slice(0, PACK), SCALAR_GROUPS[g][u])
             if g == 0:
                 nc.vector.tensor_copy(scales[:], scales_all[:].bitcast(U8).indirect(offsets[:]))
-            else:
-                load_w2()
             for u in PAIR_ORDER:
                 quantise_w1(g, u)
                 for q in range(QUARTERS):
                     first_product(g, q, u)
 
-        for u in PAIR_ORDER:
-            cast_w1(LAST, u)
+        for d in range(2):
+            for u in PAIR_ORDER:
+                cast_w1(LAST, u, w1_raw_last[d], slice(2 * d, 2 * d + 2), SCALAR_GROUPS_LAST[d][u])
         for u in PAIR_ORDER:
             quantise_w1(LAST, u)
         for q in range(QUARTERS):

@@ -33,15 +33,14 @@ UPPER, LOWER = PAIR_ORDER
 STORES = ((0, 256), (256, 384), (384, 512))
 
 SCALAR_GROUPS = ((32, 16), (26, 0))
-SCALAR_GROUPS_LAST = ((0, 32), (10, 10))
+SCALAR_GROUPS_LAST = ((8, 32), (14, 10))
 GPSIMD_TOKENS = 96
 SCALAR_SECOND_TOKENS = 32
-SCALAR_LAST_TOKENS = 80
+SCALAR_LAST_TOKENS = 96
 QUANTISE_ORDER = (1, 0, 2, 3)
 
 SCALES_ALL_KIB = 16
 W1_CODES_0_KIB = (16.5, 15.5)
-W1_BF_UPPER_KIB = 20
 W2_RAW_KIB = 1
 W2_BF_KIB = 5.5
 POSITIVE_KIB = (0, 2, 4, 6)
@@ -62,22 +61,19 @@ def tile_picked_pick_mlp_relu2_sub_p_kernel(tc, x_words, x_scales, w1, w2, offs,
 
         offsets = keep.tile([P, S // LIST_ROWS], U16, name="offsets")
         scales_all = placed_at(SCALES_ALL_KIB, "scales_all", [P, T // 4], I32)
-        words_early = kept("words_early", [P, LAST * T], I32)
-        words_last = kept("words_last", [P, T], I32)
-        words_all = [words_early[:, g * T : (g + 1) * T] for g in range(LAST)] + [words_last[:]]
+        words_all = [kept(f"words_all{g}", [P, T], I32) for g in range(PASSES)]
         w1_raw = [kept(f"w1_raw{g}", [P, PACK, H], F32) for g in range(LAST)]
         w1_raw_last = [kept(f"w1_raw_last{d}", [P, 2, H], F32) for d in range(2)]
-        w1_bf = [
+        w1_bf = [[kept(f"w1_bf{g}{u}", [P, PACK * H // PAIRS], BF16) for u in range(PAIRS)] for g in range(PASSES)]
+        codes_kib = {(0, LOWER): W1_CODES_0_KIB[LOWER], (0, UPPER): W1_CODES_0_KIB[UPPER]}
+        w1_codes = [
             [
-                placed_at(W1_BF_UPPER_KIB, f"w1_bf{g}{u}", [P, PACK * H // PAIRS], BF16)
-                if u == UPPER and g < LAST
-                else kept(f"w1_bf{g}{u}", [P, PACK * H // PAIRS], BF16)
+                placed_at(codes_kib[g, u], f"w1_codes{g}{u}", [P, H // PAIRS], U32)
+                if (g, u) in codes_kib
+                else kept(f"w1_codes{g}{u}", [P, H // PAIRS], U32)
                 for u in range(PAIRS)
             ]
             for g in range(PASSES)
-        ]
-        w1_codes = [[placed_at(kib, f"w1_codes0{u}", [P, H // PAIRS], U32) for u, kib in enumerate(W1_CODES_0_KIB)]] + [
-            [kept(f"w1_codes{g}{u}", [P, H // PAIRS], U32) for u in range(PAIRS)] for g in range(1, PASSES)
         ]
         w1_scales = [[kept(f"w1_scales{g}{u}", [P, H // PAIRS], U8) for u in range(PAIRS)] for g in range(PASSES)]
         words = [kept(f"words{g}", [P, S], U32) for g in range(PASSES)]
@@ -94,6 +90,9 @@ def tile_picked_pick_mlp_relu2_sub_p_kernel(tc, x_words, x_scales, w1, w2, offs,
         acc = [psum.tile([P, PACK, QUARTER], F32, name=f"acc{q}") for q in range(QUARTERS)]
         y = [psum.tile([P, QUARTER], F32, name=f"y{q}") for q in range(QUARTERS)]
 
+        def load_words(g):
+            nc.sync.dma_start(out=words_all[g][:], in_=x_words[g].rearrange("p c r -> p (c r)").bitcast(I32))
+
         def load_w1_last(d):
             rows = w1[LAST * K_PASS :, :].rearrange("(p j) c -> p j c", j=PACK)
             nc.sync.dma_start(out=w1_raw_last[d][:], in_=rows[:, 2 * d : 2 * d + 2, :])
@@ -102,21 +101,17 @@ def tile_picked_pick_mlp_relu2_sub_p_kernel(tc, x_words, x_scales, w1, w2, offs,
             rows = w1[g * K_PASS : (g + 1) * K_PASS, :]
             nc.sync.dma_start(out=w1_raw[g][:], in_=rows.rearrange("(p j) c -> p j c", j=PACK))
 
-        def load_w2():
-            rows = w2.rearrange("(a u l e) m -> u a l (e m)", u=PAIRS, l=4, e=2)
-            for u in range(PAIRS):
-                nc.sync.dma_start(out=w2_raw[:, 2 * u : 2 * u + 2, :].rearrange("p e m -> p (e m)"), in_=rows[u])
-
         def gather_words(g, lo, hi):
             entries = offsets[:, lo // LIST_ROWS : hi // LIST_ROWS]
-            nc.vector.tensor_copy(words[g][:, lo:hi], words_all[g].bitcast(U32).indirect(entries))
+            nc.vector.tensor_copy(words[g][:, lo:hi], words_all[g][:].bitcast(U32).indirect(entries))
 
         def cast_w1(g, u, raw, rows, split):
-            dst = w1_bf[g][u][:].rearrange("p (e a c b j) -> p a c j b e", e=2, c=2, b=2, j=PACK)[:, :, :, rows]
-            src = raw[:].rearrange("p j (a u c b e) -> p u a c j b e", u=PAIRS, c=2, b=2, e=2)[:, u]
+            dst = w1_bf[g][u][:].rearrange("p (e m j) -> p m j e", e=2, j=PACK)[:, :, rows]
+            src = raw[:].rearrange("p j (m u e) -> p u m j e", u=PAIRS, e=2)[:, u]
+            split = 4 * split
             if split > 0:
                 nc.scalar.copy(out=dst[:, :split], in_=src[:, :split])
-            if split < GROUPS:
+            if split < P:
                 nc.vector.tensor_copy(out=dst[:, split:], in_=src[:, split:])
 
         def quantise_w1(g, u):
@@ -189,11 +184,9 @@ def tile_picked_pick_mlp_relu2_sub_p_kernel(tc, x_words, x_scales, w1, w2, offs,
                 nc.sync.dma_start(out=out[:, lo:hi], in_=y_sb[r][:])
 
         nc.gpsimd.memset(scales_all[:], 0)
-        nc.sync.dma_start(
-            out=words_early[:].rearrange("p (g c) -> p g c", g=LAST),
-            in_=x_words[:LAST].rearrange("g p c r -> p g (c r)").bitcast(I32),
-        )
+        load_words(0)
         nc.sync.dma_start(offsets[:], offs)
+        load_words(1)
         load_w1(0)
         for b in range(P // QUADRANT):
             nc.sync.dma_start(
@@ -203,8 +196,8 @@ def tile_picked_pick_mlp_relu2_sub_p_kernel(tc, x_words, x_scales, w1, w2, offs,
         load_w1(1)
         for d in range(2):
             load_w1_last(d)
-        nc.sync.dma_start(out=words_last[:], in_=x_words[LAST].rearrange("p c r -> p (c r)").bitcast(I32))
-        load_w2()
+        load_words(LAST)
+        nc.sync.dma_start(out=w2_raw[:], in_=w2.rearrange("(p t) m -> p t m", t=PACK))
 
         for g in range(LAST):
             gather_words(g, 0, S)

from contextlib import ExitStack

import concourse.mybir as mybir

K, T, S, H, N = 1536, 1024, 512, 512, 128
FLOPS = 2 * K * H * S + 2 * H * N * S

F32 = mybir.dt.float32
BF16 = mybir.dt.bfloat16
I32 = mybir.dt.int32
U32 = mybir.dt.uint32
U16 = mybir.dt.uint16
U8 = mybir.dt.uint8
FP8X4 = mybir.dt.float8_e4m3fn_x4
ACT = mybir.ActivationFunctionType
ALU = mybir.AluOpType

P = 128
PACK = 4
K_PASS = P * PACK
PASSES = K // K_PASS
LAST = PASSES - 1
QUADRANT = 32
SCALE_ROWS = 4
LIST_ROWS = 16
LINE = 4
PAIRS = 2
PAIR_ORDER = (1, 0)
GROUPS = H // 16
QUARTER = 128
QUARTERS = S // QUARTER
UPPER, LOWER = PAIR_ORDER
STORES = ((0, 256), (256, 384), (384, 512))

SCALAR_GROUPS = ((32, 16), (26, 0))
SCALAR_GROUPS_LAST = ((8, 32), (14, 10))
GPSIMD_TOKENS = 96
SCALAR_SECOND_TOKENS = 32
SCALAR_LAST_TOKENS = 96
QUANTISE_ORDER = (1, 0, 2, 3)

SCALES_ALL_KIB = 16
W1_CODES_0_KIB = (16.5, 15.5)
W2_RAW_KIB = 1
W2_BF_KIB = 5.5
POSITIVE_KIB = (0, 2, 4, 6)


def tile_picked_pick_mlp_relu2_sub_p_kernel(tc, x_words, x_scales, w1, w2, offs, out):
    nc = tc.nc
    with ExitStack() as ctx:
        keep = ctx.enter_context(tc.tile_pool(name="keep", bufs=1))
        psum = ctx.enter_context(tc.psum_pool(name="psum", bufs=1))
        placed = ctx.enter_context(tc.tile_pool(name="placed", bufs=1))

        def kept(name, shape, dtype):
            return keep.tile(shape, dtype, name=name, align_bytes=64)

        def placed_at(kib, name, shape, dtype):
            return placed.tile(shape, dtype, name=name, tag=name, align_bytes=64, offset=int(1024 * kib))

        offsets = keep.tile([P, S // LIST_ROWS], U16, name="offsets")
        scales_all = placed_at(SCALES_ALL_KIB, "scales_all", [P, T // 4], I32)
        words_all = [kept(f"words_all{g}", [P, T], I32) for g in range(PASSES)]
        w1_raw = [kept(f"w1_raw{g}", [P, PACK, H], F32) for g in range(LAST)]
        w1_raw_last = [kept(f"w1_raw_last{d}", [P, 2, H], F32) for d in range(2)]
        w1_bf = [[kept(f"w1_bf{g}{u}", [P, PACK * H // PAIRS], BF16) for u in range(PAIRS)] for g in range(PASSES)]
        codes_kib = {(0, LOWER): W1_CODES_0_KIB[LOWER], (0, UPPER): W1_CODES_0_KIB[UPPER]}
        w1_codes = [
            [
                placed_at(codes_kib[g, u], f"w1_codes{g}{u}", [P, H // PAIRS], U32)
                if (g, u) in codes_kib
                else kept(f"w1_codes{g}{u}", [P, H // PAIRS], U32)
                for u in range(PAIRS)
            ]
            for g in range(PASSES)
        ]
        w1_scales = [[kept(f"w1_scales{g}{u}", [P, H // PAIRS], U8) for u in range(PAIRS)] for g in range(PASSES)]
        words = [kept(f"words{g}", [P, S], U32) for g in range(PASSES)]
        scales = kept("scales", [P, S], U8)
        w2_raw = placed_at(W2_RAW_KIB, "w2_raw", [P, PACK, N], F32)
        w2_bf = placed_at(W2_BF_KIB, "w2_bf", [P, PACK * N], BF16)
        w2_codes = kept("w2_codes", [P, N], U32)
        w2_scales = kept("w2_scales", [P, N], U8)
        positive = [placed_at(kib, f"positive{q}", [P, PACK * QUARTER], F32) for q, kib in enumerate(POSITIVE_KIB)]
        h_bf = [kept(f"h_bf{q}", [P, PACK * QUARTER], BF16) for q in range(QUARTERS)]
        h_codes = [kept(f"h_codes{q}", [P, QUARTER], U32) for q in range(QUARTERS)]
        h_scales = [kept(f"h_scales{q}", [P, QUARTER], U8) for q in range(QUARTERS)]
        y_sb = [kept(f"y_sb{r}", [P, hi - lo], F32) for r, (lo, hi) in enumerate(STORES)]
        acc = [psum.tile([P, PACK, QUARTER], F32, name=f"acc{q}") for q in range(QUARTERS)]
        y = [psum.tile([P, QUARTER], F32, name=f"y{q}") for q in range(QUARTERS)]

        def load_words(g):
            nc.sync.dma_start(out=words_all[g][:], in_=x_words[g].rearrange("p c r -> p (c r)").bitcast(I32))

        def load_w1_last(d):
            rows = w1[LAST * K_PASS :, :].rearrange("(p j) c -> p j c", j=PACK)
            nc.sync.dma_start(out=w1_raw_last[d][:], in_=rows[:, 2 * d : 2 * d + 2, :])

        def load_w1(g):
            rows = w1[g * K_PASS : (g + 1) * K_PASS, :]
            nc.sync.dma_start(out=w1_raw[g][:], in_=rows.rearrange("(p j) c -> p j c", j=PACK))

        def gather_words(g, lo, hi):
            entries = offsets[:, lo // LIST_ROWS : hi // LIST_ROWS]
            nc.vector.tensor_copy(words[g][:, lo:hi], words_all[g][:].bitcast(U32).indirect(entries))

        def cast_w1(g, u, raw, rows, split):
            dst = w1_bf[g][u][:].rearrange("p (e m j) -> p m j e", e=2, j=PACK)[:, :, rows]
            src = raw[:].rearrange("p j (m u e) -> p u m j e", u=PAIRS, e=2)[:, u]
            split = 4 * split
            if split > 0:
                nc.scalar.copy(out=dst[:, :split], in_=src[:, :split])
            if split < P:
                nc.vector.tensor_copy(out=dst[:, split:], in_=src[:, split:])

        def quantise_w1(g, u):
            nc.vector.quantize_mx(out=w1_codes[g][u][:].bitcast(FP8X4), scales=w1_scales[g][u][:], in_=w1_bf[g][u][:])

        def first_product(g, q, u):
            tokens = slice(q * QUARTER, (q + 1) * QUARTER)
            for e in range(2):
                channels = slice(e * P, (e + 1) * P)
                nc.tensor.matmul_mx(
                    out=acc[q][:, 2 * u + e, :],
                    lhsT=w1_codes[g][u][:, channels].bitcast(FP8X4),
                    lhsT_scale=w1_scales[g][u][:, channels],
                    rhs=words[g][:, tokens].bitcast(FP8X4),
                    rhs_scale=scales[SCALE_ROWS * g : P, tokens],
                    start=(g == 0 and u == PAIR_ORDER[0] and e == 0),
                    stop=(g == LAST and u == PAIR_ORDER[-1] and e == 1),
                )

        def sums_by_token(q, lo, hi):
            return acc[q][:, :, lo:hi].rearrange("p t n -> p n t")

        def by_token(tile, lo, hi):
            return tile[:, PACK * lo : PACK * hi].rearrange("p (n t) -> p n t", t=PACK)

        def relu_on_scalar(q):
            nc.scalar.activation(out=by_token(positive[q], 0, QUARTER), in_=sums_by_token(q, 0, QUARTER), func=ACT.Relu)

        def relu_on_vector(q):
            nc.vector.tensor_scalar_max(by_token(positive[q], 0, QUARTER), sums_by_token(q, 0, QUARTER), 0.0)

        def square_on_gpsimd(q, lo, hi):
            columns = slice(PACK * lo, PACK * hi)
            nc.gpsimd.tensor_tensor(h_bf[q][:, columns], positive[q][:, columns], positive[q][:, columns], ALU.mult)

        def square_on_scalar(q, lo, hi):
            columns = slice(PACK * lo, PACK * hi)
            nc.scalar.activation(out=h_bf[q][:, columns], in_=positive[q][:, columns], func=ACT.Square)

        def square_on_vector(q, lo, hi):
            nc.vector.scalar_tensor_tensor(
                by_token(h_bf[q], lo, hi),
                sums_by_token(q, lo, hi),
                0.0,
                by_token(positive[q], lo, hi),
                ALU.max,
                ALU.mult,
            )

        def second_product(q):
            nc.tensor.matmul_mx(
                out=y[q][:],
                lhsT=w2_codes[:].bitcast(FP8X4),
                lhsT_scale=w2_scales[:],
                rhs=h_codes[q][:].bitcast(FP8X4),
                rhs_scale=h_scales[q][:],
                start=True,
                stop=True,
            )

        def store(q):
            r = min(r for r, (lo, hi) in enumerate(STORES) if (q + 1) * QUARTER <= hi)
            lo, hi = STORES[r]
            dst = y_sb[r][:, q * QUARTER - lo : (q + 1) * QUARTER - lo]
            if q < QUARTERS - 1:
                nc.scalar.activation(out=dst, in_=y[q][:], func=ACT.Copy)
            else:
                nc.vector.tensor_copy(out=dst, in_=y[q][:])
            if (q + 1) * QUARTER == hi:
                nc.sync.dma_start(out=out[:, lo:hi], in_=y_sb[r][:])

        nc.gpsimd.memset(scales_all[:], 0)
        load_words(0)
        nc.sync.dma_start(offsets[:], offs)
        load_words(1)
        load_w1(0)
        for b in range(P // QUADRANT):
            nc.sync.dma_start(
                out=scales_all[QUADRANT * b : QUADRANT * b + SCALE_ROWS * PASSES, :],
                in_=x_scales[:, SCALE_ROWS * b : SCALE_ROWS * (b + 1), :].bitcast(I32),
            )
        load_w1(1)
        for d in range(2):
            load_w1_last(d)
        load_words(LAST)
        nc.sync.dma_start(out=w2_raw[:], in_=w2.rearrange("(p t) m -> p t m", t=PACK))

        for g in range(LAST):
            gather_words(g, 0, S)
        for g in range(LAST):
            for u in PAIR_ORDER:
                cast_w1(g, u, w1_raw[g], slice(0, PACK), SCALAR_GROUPS[g][u])
            if g == 0:
                nc.vector.tensor_copy(scales[:], scales_all[:].bitcast(U8).indirect(offsets[:]))
            for u in PAIR_ORDER:
                quantise_w1(g, u)
                for q in range(QUARTERS):
                    first_product(g, q, u)

        for d in range(2):
            for u in PAIR_ORDER:
                cast_w1(LAST, u, w1_raw_last[d], slice(2 * d, 2 * d + 2), SCALAR_GROUPS_LAST[d][u])
        for u in PAIR_ORDER:
            quantise_w1(LAST, u)
        for q in range(QUARTERS):
            gather_words(LAST, q * QUARTER, (q + 1) * QUARTER)
            for u in PAIR_ORDER:
                first_product(LAST, q, u)

        nc.scalar.activation(
            out=w2_bf[:].rearrange("p (c v j) -> p c j v", v=LINE, j=PACK),
            in_=w2_raw[:].rearrange("p j (c v) -> p c j v", v=LINE),
            func=ACT.Copy,
        )
        nc.vector.quantize_mx(out=w2_codes[:].bitcast(FP8X4), scales=w2_scales[:], in_=w2_bf[:])

        relu_on_scalar(0)
        relu_on_vector(1)
        square_on_gpsimd(0, 0, GPSIMD_TOKENS)
        relu_on_scalar(2)
        relu_on_vector(3)
        square_on_scalar(0, GPSIMD_TOKENS, QUARTER)
        square_on_scalar(1, 0, SCALAR_SECOND_TOKENS)
        square_on_vector(1, SCALAR_SECOND_TOKENS, QUARTER)
        square_on_scalar(2, 0, QUARTER)
        square_on_scalar(3, 0, SCALAR_LAST_TOKENS)
        square_on_vector(3, SCALAR_LAST_TOKENS, QUARTER)
        for q in QUANTISE_ORDER:
            nc.vector.quantize_mx(out=h_codes[q][:].bitcast(FP8X4), scales=h_scales[q][:], in_=h_bf[q][:])
        for q in range(QUARTERS):
            second_product(q)
            store(q)
